import numpy as np
import ml_dtypes


def mxq(x, axis, fmt="e4m3"):
    dtype, down = {"e4m3": (ml_dtypes.float8_e4m3fn, 7), "e5m2": (ml_dtypes.float8_e5m2, 14)}[fmt]
    v = np.moveaxis(np.asarray(x, np.float32).astype(ml_dtypes.bfloat16).astype(np.float64), axis, -1)
    blocks = v.reshape(v.shape[:-1] + (-1, 32))
    amax = np.abs(blocks).max(-1, keepdims=True)
    byte = np.maximum(np.where(amax > 0, np.frexp(amax)[1] - 1 + 127, 0) - down, 1)
    scale = np.exp2(byte - 127.0)
    codes = (blocks / scale).astype(np.float32).astype(dtype).astype(np.float64)
    return np.moveaxis((codes * scale).reshape(v.shape), -1, axis)


WIDE = False


def mx_kscale(k):
    if not WIDE:
        return np.ones(k)
    levels = np.array([24, -24, 12, -12, 0])
    if k % 512:
        return np.exp2(np.random.permutation(np.resize(levels, k // 32))).repeat(32)
    a = np.empty((k // 512, 16))
    for p in range(k // 512):
        a[p, :8] = np.random.permutation(np.resize(levels, 8))
        for g in range(8):
            far = levels[np.abs(levels - a[p, g]) >= 10]
            a[p, g + 8] = far[np.random.randint(len(far))]
    return np.exp2(a.ravel()).repeat(32)


def f64(x):
    return np.asarray(x).astype(np.float64)


def striped(idx):
    return np.tile(idx.reshape(-1, 16).T, (8, 1)).astype(np.uint16)


def unstriped(offs):
    return offs[:16].T.reshape(-1).astype(np.int64)


E2M1 = np.array([0.0, 0.5, 1.0, 1.5, 2.0, 3.0, 4.0, 6.0, -0.0, -0.5, -1.0, -1.5, -2.0, -3.0, -4.0, -6.0])


def pack_weight(w, fmt):
    k, n = w.shape
    w = f64(np.asarray(w, np.float32).astype(ml_dtypes.bfloat16)).reshape(k // 32, 32, n)
    amax = np.abs(w).max(1)
    if fmt == "e4m3":
        byte = np.frexp(amax)[1] - 1 + 127 - 7
    else:
        mant, ex = np.frexp(amax / 6.0)
        byte = np.where(mant > 0.5, ex, ex - 1) + 127
    byte = np.clip(np.where(amax > 0, byte, 1), 1, 254)
    scaled = (w * np.exp2(127.0 - byte)[:, None, :]).reshape(k, n).astype(np.float32)
    by_word = np.ascontiguousarray(scaled.reshape(k // 512, 128, 4, n).transpose(0, 1, 3, 2))
    if fmt == "e4m3":
        words = by_word.astype(ml_dtypes.float8_e4m3fn).view(np.uint8)
    else:
        c = by_word.astype(ml_dtypes.float4_e2m1fn).view(np.uint8) & 0xF
        words = (c[..., 0::2] | (c[..., 1::2] << 4)).reshape(k // 512, 128, 2 * n)
    return np.ascontiguousarray(words), np.ascontiguousarray(byte.astype(np.uint8).reshape(k // 512, 16, n))


def unpack_weight(words, scales, fmt):
    g, _, n = scales.shape
    words = np.ascontiguousarray(words).reshape(g, 128, n, -1)
    if fmt == "e4m3":
        vals = words.view(ml_dtypes.float8_e4m3fn).astype(np.float64)
    else:
        nib = np.empty((g, 128, n, 4), np.uint8)
        nib[..., 0::2] = words & 0xF
        nib[..., 1::2] = words >> 4
        vals = E2M1[nib]
    vals = vals * np.repeat(np.exp2(scales.astype(np.float64) - 127.0), 8, axis=1)[..., None]
    return vals.transpose(0, 1, 3, 2).reshape(g * 512, n)


def pack_table4(v):
    words, scales = pack_weight(v, "e2m1")
    g, t = words.shape[0] // 2, v.shape[1]
    return np.ascontiguousarray(words.reshape(g, 2, 128, t, 2).transpose(0, 2, 3, 1, 4).reshape(g, 128, t, 4)), scales


def unpack_table4(words, scales):
    g, _, t, _ = words.shape
    return unpack_weight(words.reshape(g, 128, t, 2, 2).transpose(0, 3, 1, 2, 4).reshape(2 * g, 128, 2 * t), scales, "e2m1")


def sigm(f):
    return 1.0 / (1.0 + np.exp(-np.maximum(f, -700.0)))


K, N, T, J = 1024, 256, 1024, 512


def setup_inputs():
    n = np.random.standard_normal
    s = mx_kscale(K)[:, None]
    p_tab = pack_table4(n((K, T)) * s)
    p_wk4 = pack_weight(n((K, N)) / np.sqrt(K) / s, "e2m1")
    return {
        "tab_words": p_tab[0],
        "tab_scales": p_tab[1],
        "wk4_words": p_wk4[0],
        "wk4_scales": p_wk4[1],
        "wkd": (0.4 * (n((K, N)) / np.sqrt(K) / s)).astype(np.float32),
        "wv": (n((K, N)) / np.sqrt(K) / s).astype(np.float32),
        "st": (n((N, J))).astype(np.float32),
        "rT": (n((N, T))).astype(np.float32),
        "offs": striped(np.random.permutation(T)[:J]),
    }


def reference(tab_words, tab_scales, wk4_words, wk4_scales, wkd, wv, st, rT, offs):
    idx = unstriped(offs)
    tab_ = unpack_table4(tab_words, tab_scales)[:, idx]
    wk4_ = unpack_weight(wk4_words, wk4_scales, "e2m1")
    wkd_ = mxq(f64(wkd), 0, "e4m3")
    wv_q_ = mxq(f64(wv), 0, "e4m3")
    wv_r_ = mxq(f64(wv) - wv_q_, 0, "e4m3")
    ke = wk4_.T @ tab_ + wkd_.T @ tab_
    ve = wv_q_.T @ tab_ + wv_r_.T @ tab_
    gate = sigm(ke + f64(st))
    return f64(rT)[:, idx] + gate * ve

@@ -1,0 +1,204 @@
+from contextlib import ExitStack
+
+import concourse.mybir as mybir
+from concourse.masks import make_identity
+
+K, N, T, J = 1024, 256, 1024, 512
+FLOPS = 1342177280
+
+F32 = mybir.dt.float32
+BF16 = mybir.dt.bfloat16
+I32 = mybir.dt.int32
+U32 = mybir.dt.uint32
+U16 = mybir.dt.uint16
+U8 = mybir.dt.uint8
+FP8X4 = mybir.dt.float8_e4m3fn_x4
+FP4X4 = mybir.dt.float4_e2m1fn_x4
+ALU = mybir.AluOpType
+ACT = mybir.ActivationFunctionType
+
+P = 128
+PACK = 4
+K_PASS = P * PACK
+PASSES = K // K_PASS
+HALVES = N // P
+
+
+def tile_list_engram_dl_tier_addL_kernel(
+    tc, tab_words, tab_scales, wk4_words, wk4_scales, wkd, wv, st, rT, offs, out
+):
+    nc = tc.nc
+    with ExitStack() as ctx:
+        sb = ctx.enter_context(tc.tile_pool(name="sb", bufs=1))
+        ps = ctx.enter_context(tc.psum_pool(name="ps", bufs=1))
+
+        def tile(name, shape, dtype):
+            return sb.tile(shape, dtype, name=name, align_bytes=64)
+
+        offsets = sb.tile([P, J // 16], U16, name="offsets")
+        nc.sync.dma_start(offsets[:], offs)
+
+        tab_sc = tile("tab_sc", [P, PASSES, T // 4], I32)
+        nc.vector.memset(tab_sc[:], 0)
+        for q in range(4):
+            nc.sync.dma_start(
+                tab_sc[32 * q : 32 * q + 4, :, :],
+                tab_scales.bitcast(I32)[:, 4 * q : 4 * q + 4, :].rearrange("a r t -> r a t"),
+            )
+        tab_w = tile("tab_w", [P, T], I32)
+        nc.sync.dma_start(tab_w[:], tab_words[0].rearrange("p t b -> p (t b)").bitcast(I32))
+
+        def load_weight(name, w, a):
+            raw = tile("%s_raw%d" % (name, a), [P, PACK, N], F32)
+            nc.sync.dma_start(
+                raw[:], w[a * K_PASS : (a + 1) * K_PASS, :].rearrange("(p i) n -> p i n", i=PACK)
+            )
+            return raw
+
+        wv_raw = [load_weight("wv", wv, a) for a in range(PASSES)]
+        wkd_raw = [load_weight("wkd", wkd, a) for a in range(PASSES)]
+
+        wk4_sc = tile("wk4_sc", [P, PASSES, N // 4], I32)
+        nc.vector.memset(wk4_sc[:], 0)
+        for q in range(4):
+            nc.sync.dma_start(
+                wk4_sc[32 * q : 32 * q + 4, :, :],
+                wk4_scales.bitcast(I32)[:, 4 * q : 4 * q + 4, :].rearrange("a r c -> r a c"),
+            )
+        wk4_w = tile("wk4_w", [P, PASSES, 2 * N // 4], I32)
+        nc.sync.dma_start(wk4_w[:], wk4_words.bitcast(I32).rearrange("a p c -> p a c"))
+        st_sb = tile("st_sb", [P, HALVES, J], F32)
+        nc.sync.dma_start(st_sb[:], st.rearrange("(h p) j -> p h j", p=P))
+        rec = []
+        for h in range(HALVES):
+            r = tile("rec%d" % h, [P, T], F32)
+            nc.sync.dma_start(r[:], rT[h * P : (h + 1) * P, :])
+            rec.append(r)
+
+        warm = tile("warm", [P, 1], F32)
+        warm2 = tile("warm2", [P, 1], F32)
+        nc.gpsimd.memset(warm[:], 0.0)
+        nc.scalar.activation(warm2[:], warm[:], ACT.Sigmoid)
+
+        eye = tile("eye", [P, P], BF16)
+        make_identity(nc, eye[:])
+        pick_in = tile("pick_in", [P, PACK * (K_PASS + 1)], BF16)
+        nc.vector.memset(pick_in[:], 0.0)
+        nc.vector.tensor_copy(
+            pick_in[:].rearrange("p (i r) -> p i r", i=PACK)[:, :, 0:K_PASS:PACK],
+            eye[:].unsqueeze(1).to_broadcast([P, PACK, P]),
+        )
+        pick_w = tile("pick_w", [P, PACK * P], U32)
+        pick_sc = tile("pick_sc", [P, PACK * P], U8)
+        nc.vector.quantize_mx(pick_w[:].bitcast(FP8X4), pick_sc[:], pick_in[:, 0 : PACK * K_PASS])
+
+        got_sc = tile("got_sc", [P, PASSES, J], U8)
+        for a in range(PASSES):
+            nc.vector.tensor_copy(got_sc[:, a, :], tab_sc[:, a, :].bitcast(U8).indirect(offsets[:]))
+        got_w = tile("got_w", [P, J], I32)
+        nc.vector.tensor_copy(got_w[:].bitcast(U32), tab_w[:].bitcast(U32).indirect(offsets[:]))
+        v_w = tile("v_w", [P, PASSES, 2 * J], U8)
+        nc.vector.tensor_copy(
+            v_w[:].bitcast(U16), got_w[:].bitcast(U16).rearrange("p (j d) -> p d j", d=PASSES)
+        )
+
+        def interleaved(grouped):
+            return grouped.rearrange("p (c u t) -> p c t u", u=4, t=PACK)
+
+        def planes(raw):
+            return raw.rearrange("p t (c u) -> p c t u", u=4)
+
+        def cast(name, raw):
+            grouped = tile(name, [P, PACK * N], BF16)
+            nc.scalar.copy(interleaved(grouped[:]), planes(raw[:]))
+            return grouped
+
+        def table_pass(acc, words, scales, a, start, stop):
+            nc.tensor.matmul_mx(
+                acc[:], lhsT=words, lhsT_scale=scales,
+                rhs=v_w[:, a, :].bitcast(FP4X4), rhs_scale=got_sc[:, a, :],
+                start=start, stop=stop,
+            )
+
+        ke = [ps.tile([P, J], F32, name="ke%d" % h) for h in range(HALVES)]
+        ve = [ps.tile([P, J], F32, name="ve%d" % h) for h in range(HALVES)]
+
+        wv_bf = [cast("wv_bf%d" % a, wv_raw[a]) for a in range(PASSES)]
+        wkd_bf = [cast("wkd_bf%d" % a, wkd_raw[a]) for a in range(PASSES)]
+
+        def quantise(name, grouped):
+            words = tile(name + "_w", [P, N], U32)
+            scales = tile(name + "_sc", [P, N], U8)
+            nc.vector.quantize_mx(words[:].bitcast(FP8X4), scales[:], grouped)
+            return words, scales
+
+        wq = [quantise("wq%d" % a, wv_bf[a][:]) for a in range(PASSES)]
+        back = {}
+        for a in range(PASSES):
+            for h in range(HALVES):
+                cols = slice(h * P, (h + 1) * P)
+                bank = ps.tile([P, PACK, P], F32, name="back%d%d" % (h, a))
+                for i in range(PACK):
+                    sel = slice(i * P, (i + 1) * P)
+                    nc.tensor.matmul_mx(
+                        bank[:, i, :], lhsT=pick_w[:, sel].bitcast(FP8X4), lhsT_scale=pick_sc[:, sel],
+                        rhs=wq[a][0][:, cols].bitcast(FP8X4), rhs_scale=wq[a][1][:, cols],
+                        start=True, stop=True,
+                    )
+                back[h, a] = bank
+        for h in range(HALVES):
+            cols = slice(h * P, (h + 1) * P)
+            for a in range(PASSES):
+                table_pass(ve[h], wq[a][0][:, cols].bitcast(FP8X4), wq[a][1][:, cols], a, a == 0, False)
+        for h in range(HALVES):
+            for a in range(PASSES):
+                table_pass(
+                    ke[h],
+                    wk4_w[:, a, 64 * h : 64 * (h + 1)].bitcast(FP4X4),
+                    wk4_sc[:, a, 32 * h : 32 * (h + 1)].bitcast(U8),
+                    a, a == 0, False,
+                )
+
+        left = [tile("left%d" % a, [P, HALVES, PACK * P], BF16) for a in range(PASSES)]
+
+        def leftover(a, h):
+            cols = slice(h * P, (h + 1) * P)
+            nc.vector.tensor_tensor(
+                interleaved(left[a][:, h, :]), planes(wv_raw[a][:, :, cols]), planes(back[h, a][:]),
+                ALU.subtract,
+            )
+
+        leftover(0, 0)
+        leftover(0, 1)
+        wd = [quantise("wd0", wkd_bf[0][:])]
+        leftover(1, 0)
+        wr = [quantise("wr0", left[0][:].rearrange("p h c -> p (h c)"))]
+        leftover(1, 1)
+        wd.append(quantise("wd1", wkd_bf[1][:]))
+        wr.append(quantise("wr1", left[1][:].rearrange("p h c -> p (h c)")))
+
+        for a in range(PASSES):
+            for acc, w in ((ke, wd), (ve, wr)):
+                for h in range(HALVES):
+                    cols = slice(h * P, (h + 1) * P)
+                    table_pass(acc[h], w[a][0][:, cols].bitcast(FP8X4), w[a][1][:, cols], a, False, a == PASSES - 1)
+
+        got_rec, gate = [], []
+        for h in range(HALVES):
+            g = tile("got_rec%d" % h, [P, J], F32)
+            nc.vector.tensor_copy(g[:], rec[h][:].indirect(offsets[:]))
+            got_rec.append(g)
+            pre = tile("pre%d" % h, [P, J], F32)
+            nc.vector.tensor_tensor(pre[:], ke[h][:], st_sb[:, h, :], ALU.add)
+            gt = tile("gate%d" % h, [P, J], F32)
+            nc.scalar.activation(gt[:], pre[:], ACT.Sigmoid)
+            gate.append(gt)
+        passed = []
+        for h in range(HALVES):
+            pt = tile("passed%d" % h, [P, J], F32)
+            nc.vector.tensor_tensor(pt[:], ve[h][:], gate[h][:], ALU.mult)
+            passed.append(pt)
+        for h in range(HALVES):
+            res = tile("res%d" % h, [P, J], F32)
+            nc.vector.tensor_tensor(res[:], passed[h][:], got_rec[h][:], ALU.add)
+            nc.sync.dma_start(out[h * P : (h + 1) * P, :], res[:])

@@ -1,7 +1,6 @@
 from contextlib import ExitStack
 
 import concourse.mybir as mybir
-from concourse.masks import make_identity
 
 K, N, T, J = 1024, 256, 1024, 512
 FLOPS = 1342177280
@@ -35,72 +34,62 @@ def tile_list_engram_dl_tier_addL_kernel(
         def tile(name, shape, dtype):
             return sb.tile(shape, dtype, name=name, align_bytes=64)
 
-        offsets = sb.tile([P, J // 16], U16, name="offsets")
-        nc.sync.dma_start(offsets[:], offs)
-
-        tab_sc = tile("tab_sc", [P, PASSES, T // 4], I32)
-        nc.vector.memset(tab_sc[:], 0)
-        for q in range(4):
-            nc.sync.dma_start(
-                tab_sc[32 * q : 32 * q + 4, :, :],
-                tab_scales.bitcast(I32)[:, 4 * q : 4 * q + 4, :].rearrange("a r t -> r a t"),
-            )
-        tab_w = tile("tab_w", [P, T], I32)
-        nc.sync.dma_start(tab_w[:], tab_words[0].rearrange("p t b -> p (t b)").bitcast(I32))
-
-        def load_weight(name, w, a):
-            raw = tile("%s_raw%d" % (name, a), [P, PACK, N], F32)
-            nc.sync.dma_start(
-                raw[:], w[a * K_PASS : (a + 1) * K_PASS, :].rearrange("(p i) n -> p i n", i=PACK)
-            )
+        def load_weight(name, w):
+            raw = []
+            for a in range(PASSES):
+                raw.append(tile("%s_raw%d" % (name, a), [P, PACK, N], F32))
+                nc.sync.dma_start(
+                    raw[a][:], w[a * K_PASS : (a + 1) * K_PASS, :].rearrange("(p i) n -> p i n", i=PACK)
+                )
             return raw
 
-        wv_raw = [load_weight("wv", wv, a) for a in range(PASSES)]
-        wkd_raw = [load_weight("wkd", wkd, a) for a in range(PASSES)]
+        def load_scales(name, src, queue):
+            plane = tile(name, [P, PASSES, src.shape[2] // 4], I32)
+            nc.gpsimd.memset(plane[:], 0)
+            for q in range(4):
+                queue.dma_start(
+                    plane[32 * q : 32 * q + 4, :, :],
+                    src.bitcast(I32)[:, 4 * q : 4 * q + 4, :].rearrange("a r c -> r a c"),
+                )
+            return plane
 
-        wk4_sc = tile("wk4_sc", [P, PASSES, N // 4], I32)
-        nc.vector.memset(wk4_sc[:], 0)
-        for q in range(4):
-            nc.sync.dma_start(
-                wk4_sc[32 * q : 32 * q + 4, :, :],
-                wk4_scales.bitcast(I32)[:, 4 * q : 4 * q + 4, :].rearrange("a r c -> r a c"),
-            )
+        offsets = sb.tile([P, J // 16], U16, name="offsets")
+        nc.sync.dma_start(offsets[:], offs)
+        tab_w = tile("tab_w", [P, T], I32)
+        nc.sync.dma_start(tab_w[:], tab_words[0].rearrange("p t b -> p (t b)").bitcast(I32))
+        wv_raw = load_weight("wv", wv)
+        tab_sc = load_scales("tab_sc", tab_scales, nc.scalar)
+        wkd_raw = load_weight("wkd", wkd)
+        wk4_sc = load_scales("wk4_sc", wk4_scales, nc.sync)
         wk4_w = tile("wk4_w", [P, PASSES, 2 * N // 4], I32)
         nc.sync.dma_start(wk4_w[:], wk4_words.bitcast(I32).rearrange("a p c -> p a c"))
+        rec = [tile("rec%d" % h, [P, T], F32) for h in range(HALVES)]
+        nc.sync.dma_start(rec[0][:], rT[0:P, :])
         st_sb = tile("st_sb", [P, HALVES, J], F32)
         nc.sync.dma_start(st_sb[:], st.rearrange("(h p) j -> p h j", p=P))
-        rec = []
-        for h in range(HALVES):
-            r = tile("rec%d" % h, [P, T], F32)
-            nc.sync.dma_start(r[:], rT[h * P : (h + 1) * P, :])
-            rec.append(r)
+        nc.sync.dma_start(rec[1][:], rT[P : 2 * P, :])
 
+        ones = tile("ones", [P, 32], F32)
+        nc.vector.memset(ones[:], 1.0)
         warm = tile("warm", [P, 1], F32)
-        warm2 = tile("warm2", [P, 1], F32)
-        nc.gpsimd.memset(warm[:], 0.0)
-        nc.scalar.activation(warm2[:], warm[:], ACT.Sigmoid)
-
-        eye = tile("eye", [P, P], BF16)
-        make_identity(nc, eye[:])
+        nc.scalar.activation(warm[:], ones[:, 0:1], ACT.Sigmoid)
+        count = tile("count", [P, 32], F32)
+        nc.vector.tensor_tensor_scan(count[:], ones[:], ones[:], 0.0, ALU.mult, ALU.add)
         pick_in = tile("pick_in", [P, PACK * (K_PASS + 1)], BF16)
-        nc.vector.memset(pick_in[:], 0.0)
-        nc.vector.tensor_copy(
-            pick_in[:].rearrange("p (i r) -> p i r", i=PACK)[:, :, 0:K_PASS:PACK],
-            eye[:].unsqueeze(1).to_broadcast([P, PACK, P]),
-        )
+        nc.vector.memset(pick_in[:].bitcast(I32), 0)
+        own = tile("own", [P, 32], F32)
+        nc.vector.transpose(own[:], count[:])
+        diagonals = pick_in[:].rearrange("p (i r) -> p i r", i=PACK)
+        for b in range(4):
+            rows = slice(32 * b, 32 * (b + 1))
+            nc.vector.tensor_scalar(
+                diagonals[rows, :, P * b : P * (b + 1) : PACK],
+                count[rows, :].unsqueeze(1).to_broadcast([32, PACK, 32]),
+                own[rows, 0:1], None, ALU.is_equal,
+            )
         pick_w = tile("pick_w", [P, PACK * P], U32)
         pick_sc = tile("pick_sc", [P, PACK * P], U8)
         nc.vector.quantize_mx(pick_w[:].bitcast(FP8X4), pick_sc[:], pick_in[:, 0 : PACK * K_PASS])
-
-        got_sc = tile("got_sc", [P, PASSES, J], U8)
-        for a in range(PASSES):
-            nc.vector.tensor_copy(got_sc[:, a, :], tab_sc[:, a, :].bitcast(U8).indirect(offsets[:]))
-        got_w = tile("got_w", [P, J], I32)
-        nc.vector.tensor_copy(got_w[:].bitcast(U32), tab_w[:].bitcast(U32).indirect(offsets[:]))
-        v_w = tile("v_w", [P, PASSES, 2 * J], U8)
-        nc.vector.tensor_copy(
-            v_w[:].bitcast(U16), got_w[:].bitcast(U16).rearrange("p (j d) -> p d j", d=PASSES)
-        )
 
         def interleaved(grouped):
             return grouped.rearrange("p (c u t) -> p c t u", u=4, t=PACK)
@@ -109,47 +98,85 @@ def tile_list_engram_dl_tier_addL_kernel(
             return raw.rearrange("p t (c u) -> p c t u", u=4)
 
         def cast(name, raw):
-            grouped = tile(name, [P, PACK * N], BF16)
-            nc.scalar.copy(interleaved(grouped[:]), planes(raw[:]))
+            grouped = tile(name, [P, PASSES, PACK * N], BF16)
+            for a in range(PASSES):
+                nc.scalar.copy(interleaved(grouped[:, a, :]), planes(raw[a][:]))
             return grouped
 
-        def table_pass(acc, words, scales, a, start, stop):
-            nc.tensor.matmul_mx(
-                acc[:], lhsT=words, lhsT_scale=scales,
-                rhs=v_w[:, a, :].bitcast(FP4X4), rhs_scale=got_sc[:, a, :],
-                start=start, stop=stop,
-            )
+        def quantise(name, grouped):
+            words = tile(name + "_w", [P, PASSES * N], U32)
+            scales = tile(name + "_sc", [P, PASSES * N], U8)
+            nc.vector.quantize_mx(words[:].bitcast(FP8X4), scales[:], grouped[:].rearrange("p a c -> p (a c)"))
+            return words, scales
+
+        wv_bf = cast("wv_bf", wv_raw)
+        wkd_bf = cast("wkd_bf", wkd_raw)
+
+        got_w = tile("got_w", [P, J], I32)
+        nc.vector.tensor_copy(got_w[:].bitcast(U32), tab_w[:].bitcast(U32).indirect(offsets[:]))
+        v_w = tile("v_w", [P, PASSES, 2 * J], U8)
+        nc.vector.tensor_copy(
+            v_w[:].bitcast(U16), got_w[:].bitcast(U16).rearrange("p (j d) -> p d j", d=PASSES)
+        )
+        v_sc = [tile("v_sc%d" % a, [P, J], U8) for a in range(PASSES)]
+
+        def gather_scales(a):
+            nc.vector.tensor_copy(v_sc[a][:], tab_sc[:, a, :].bitcast(U8).indirect(offsets[:]))
 
         ke = [ps.tile([P, J], F32, name="ke%d" % h) for h in range(HALVES)]
         ve = [ps.tile([P, J], F32, name="ve%d" % h) for h in range(HALVES)]
 
-        wv_bf = [cast("wv_bf%d" % a, wv_raw[a]) for a in range(PASSES)]
-        wkd_bf = [cast("wkd_bf%d" % a, wkd_raw[a]) for a in range(PASSES)]
+        def table_pass(acc, words, scales, a, start, stop):
+            nc.tensor.matmul_mx(
+                acc[:], lhsT=words, lhsT_scale=scales,
+                rhs=v_w[:, a, :].bitcast(FP4X4), rhs_scale=v_sc[a][:],
+                start=start, stop=stop,
+            )
 
-        def quantise(name, grouped):
-            words = tile(name + "_w", [P, N], U32)
-            scales = tile(name + "_sc", [P, N], U8)
-            nc.vector.quantize_mx(words[:].bitcast(FP8X4), scales[:], grouped)
-            return words, scales
+        def columns(a, h):
+            return slice(a * N + h * P, a * N + (h + 1) * P)
 
-        wq = [quantise("wq%d" % a, wv_bf[a][:]) for a in range(PASSES)]
-        back = {}
-        for a in range(PASSES):
+        def fp8_passes(acc, w, order, first, last):
             for h in range(HALVES):
-                cols = slice(h * P, (h + 1) * P)
-                bank = ps.tile([P, PACK, P], F32, name="back%d%d" % (h, a))
+                for a in order:
+                    cols = columns(a, h)
+                    table_pass(acc[h], w[0][:, cols].bitcast(FP8X4), w[1][:, cols], a,
+                               first and a == order[0], last and a == order[-1])
+
+        wq = (tile("wq_w", [P, PASSES * N], U32), tile("wq_sc", [P, PASSES * N], U8))
+        back = {}
+
+        def first_tier(a):
+            cols = slice(a * N, (a + 1) * N)
+            nc.vector.quantize_mx(wq[0][:, cols].bitcast(FP8X4), wq[1][:, cols], wv_bf[:, a, :])
+            for h in range(HALVES):
+                cols = columns(a, h)
+                bank = ps.tile([P, PACK, P], F32, name="back%d%d" % (a, h))
                 for i in range(PACK):
                     sel = slice(i * P, (i + 1) * P)
                     nc.tensor.matmul_mx(
                         bank[:, i, :], lhsT=pick_w[:, sel].bitcast(FP8X4), lhsT_scale=pick_sc[:, sel],
-                        rhs=wq[a][0][:, cols].bitcast(FP8X4), rhs_scale=wq[a][1][:, cols],
+                        rhs=wq[0][:, cols].bitcast(FP8X4), rhs_scale=wq[1][:, cols],
                         start=True, stop=True,
                     )
-                back[h, a] = bank
-        for h in range(HALVES):
-            cols = slice(h * P, (h + 1) * P)
-            for a in range(PASSES):
-                table_pass(ve[h], wq[a][0][:, cols].bitcast(FP8X4), wq[a][1][:, cols], a, a == 0, False)
+                back[a, h] = bank
+
+        left = tile("left", [P, PASSES, PACK * N], BF16)
+
+        def leftover(a):
+            for h in range(HALVES):
+                nc.vector.tensor_tensor(
+                    interleaved(left[:, a, h * K_PASS : (h + 1) * K_PASS]),
+                    planes(wv_raw[a][:, :, h * P : (h + 1) * P]), planes(back[a, h][:]),
+                    ALU.subtract,
+                )
+
+        first_tier(0)
+        gather_scales(0)
+        first_tier(1)
+        leftover(0)
+        gather_scales(1)
+        leftover(1)
         for h in range(HALVES):
             for a in range(PASSES):
                 table_pass(
@@ -158,47 +185,26 @@ def tile_list_engram_dl_tier_addL_kernel(
                     wk4_sc[:, a, 32 * h : 32 * (h + 1)].bitcast(U8),
                     a, a == 0, False,
                 )
+        wd = quantise("wd", wkd_bf)
+        fp8_passes(ke, wd, (0, 1), False, True)
+        fp8_passes(ve, wq, (0, 1), True, False)
+        wr = quantise("wr", left)
+        fp8_passes(ve, wr, (0, 1), False, True)
 
-        left = [tile("left%d" % a, [P, HALVES, PACK * P], BF16) for a in range(PASSES)]
-
-        def leftover(a, h):
-            cols = slice(h * P, (h + 1) * P)
-            nc.vector.tensor_tensor(
-                interleaved(left[a][:, h, :]), planes(wv_raw[a][:, :, cols]), planes(back[h, a][:]),
-                ALU.subtract,
-            )
-
-        leftover(0, 0)
-        leftover(0, 1)
-        wd = [quantise("wd0", wkd_bf[0][:])]
-        leftover(1, 0)
-        wr = [quantise("wr0", left[0][:].rearrange("p h c -> p (h c)"))]
-        leftover(1, 1)
-        wd.append(quantise("wd1", wkd_bf[1][:]))
-        wr.append(quantise("wr1", left[1][:].rearrange("p h c -> p (h c)")))
-
-        for a in range(PASSES):
-            for acc, w in ((ke, wd), (ve, wr)):
-                for h in range(HALVES):
-                    cols = slice(h * P, (h + 1) * P)
-                    table_pass(acc[h], w[a][0][:, cols].bitcast(FP8X4), w[a][1][:, cols], a, False, a == PASSES - 1)
-
-        got_rec, gate = [], []
+        got_rec = [tile("got_rec%d" % h, [P, J], F32) for h in range(HALVES)]
+        gate = [tile("gate%d" % h, [P, J], F32) for h in range(HALVES)]
+        nc.vector.tensor_copy(got_rec[0][:], rec[0][:].indirect(offsets[:]))
         for h in range(HALVES):
-            g = tile("got_rec%d" % h, [P, J], F32)
-            nc.vector.tensor_copy(g[:], rec[h][:].indirect(offsets[:]))
-            got_rec.append(g)
             pre = tile("pre%d" % h, [P, J], F32)
             nc.vector.tensor_tensor(pre[:], ke[h][:], st_sb[:, h, :], ALU.add)
-            gt = tile("gate%d" % h, [P, J], F32)
-            nc.scalar.activation(gt[:], pre[:], ACT.Sigmoid)
-            gate.append(gt)
+            nc.scalar.activation(gate[h][:], pre[:], ACT.Sigmoid)
+        nc.vector.tensor_copy(got_rec[1][:], rec[1][:].indirect(offsets[:]))
         passed = []
         for h in range(HALVES):
             pt = tile("passed%d" % h, [P, J], F32)
             nc.vector.tensor_tensor(pt[:], ve[h][:], gate[h][:], ALU.mult)
             passed.append(pt)
-        for h in range(HALVES):
-            res = tile("res%d" % h, [P, J], F32)
-            nc.vector.tensor_tensor(res[:], passed[h][:], got_rec[h][:], ALU.add)
-            nc.sync.dma_start(out[h * P : (h + 1) * P, :], res[:])
+        for h, lo, hi in ((0, 0, J), (1, 0, J // 2), (1, J // 2, J)):
+            res = tile("res%d_%d" % (h, lo), [P, hi - lo], F32)
+            nc.vector.tensor_tensor(res[:], passed[h][:, lo:hi], got_rec[h][:, lo:hi], ALU.add)
+            nc.sync.dma_start(out[h * P : (h + 1) * P, lo:hi], res[:])

@@ -31,65 +31,65 @@ def tile_list_engram_dl_tier_addL_kernel(
         sb = ctx.enter_context(tc.tile_pool(name="sb", bufs=1))
         ps = ctx.enter_context(tc.psum_pool(name="ps", bufs=1))
 
-        def tile(name, shape, dtype):
-            return sb.tile(shape, dtype, name=name, align_bytes=64)
+        def tile(name, shape, dtype, tag=""):
+            return sb.tile(shape, dtype, name=name, tag=tag or name, align_bytes=64)
 
-        def load_weight(name, w):
-            raw = []
-            for a in range(PASSES):
-                raw.append(tile("%s_raw%d" % (name, a), [P, PACK, N], F32))
-                nc.sync.dma_start(
-                    raw[a][:], w[a * K_PASS : (a + 1) * K_PASS, :].rearrange("(p i) n -> p i n", i=PACK)
-                )
-            return raw
-
-        def load_scales(name, src, queue):
-            plane = tile(name, [P, PASSES, src.shape[2] // 4], I32)
-            nc.gpsimd.memset(plane[:], 0)
+        def load_scales(plane, src):
             for q in range(4):
-                queue.dma_start(
+                nc.sync.dma_start(
                     plane[32 * q : 32 * q + 4, :, :],
                     src.bitcast(I32)[:, 4 * q : 4 * q + 4, :].rearrange("a r c -> r a c"),
                 )
-            return plane
 
         offsets = sb.tile([P, J // 16], U16, name="offsets")
         nc.sync.dma_start(offsets[:], offs)
-        tab_w = tile("tab_w", [P, T], I32)
-        nc.sync.dma_start(tab_w[:], tab_words[0].rearrange("p t b -> p (t b)").bitcast(I32))
-        wv_raw = load_weight("wv", wv)
-        tab_sc = load_scales("tab_sc", tab_scales, nc.scalar)
-        wkd_raw = load_weight("wkd", wkd)
-        wk4_sc = load_scales("wk4_sc", wk4_scales, nc.sync)
-        wk4_w = tile("wk4_w", [P, PASSES, 2 * N // 4], I32)
-        nc.sync.dma_start(wk4_w[:], wk4_words.bitcast(I32).rearrange("a p c -> p a c"))
-        rec = [tile("rec%d" % h, [P, T], F32) for h in range(HALVES)]
-        nc.sync.dma_start(rec[0][:], rT[0:P, :])
-        st_sb = tile("st_sb", [P, HALVES, J], F32)
-        nc.sync.dma_start(st_sb[:], st.rearrange("(h p) j -> p h j", p=P))
-        nc.sync.dma_start(rec[1][:], rT[P : 2 * P, :])
+        tab_sc = tile("tab_sc", [P, PASSES, T // 4], I32)
+        nc.gpsimd.memset(tab_sc[:], 0)
 
+        eye = tile("eye", [P, 32], F32)
         ones = tile("ones", [P, 32], F32)
         nc.vector.memset(ones[:], 1.0)
-        warm = tile("warm", [P, 1], F32)
-        nc.scalar.activation(warm[:], ones[:, 0:1], ACT.Sigmoid)
         count = tile("count", [P, 32], F32)
         nc.vector.tensor_tensor_scan(count[:], ones[:], ones[:], 0.0, ALU.mult, ALU.add)
         pick_in = tile("pick_in", [P, PACK * (K_PASS + 1)], BF16)
         nc.vector.memset(pick_in[:].bitcast(I32), 0)
         own = tile("own", [P, 32], F32)
         nc.vector.transpose(own[:], count[:])
+        nc.vector.tensor_tensor(eye[:], count[:], own[:], ALU.is_equal)
+
+        warm = tile("warm", [P, 1], F32)
+        nc.scalar.activation(warm[:], eye[:, 0:1], ACT.Sigmoid)
         diagonals = pick_in[:].rearrange("p (i r) -> p i r", i=PACK)
         for b in range(4):
             rows = slice(32 * b, 32 * (b + 1))
-            nc.vector.tensor_scalar(
+            nc.scalar.copy(
                 diagonals[rows, :, P * b : P * (b + 1) : PACK],
-                count[rows, :].unsqueeze(1).to_broadcast([32, PACK, 32]),
-                own[rows, 0:1], None, ALU.is_equal,
+                eye[rows, :].unsqueeze(1).to_broadcast([32, PACK, 32]),
             )
-        pick_w = tile("pick_w", [P, PACK * P], U32)
-        pick_sc = tile("pick_sc", [P, PACK * P], U8)
-        nc.vector.quantize_mx(pick_w[:].bitcast(FP8X4), pick_sc[:], pick_in[:, 0 : PACK * K_PASS])
+
+        def load_weight(name, w, a):
+            raw = tile("%s_raw%d" % (name, a), [P, PACK, N], F32)
+            nc.sync.dma_start(
+                raw[:], w[a * K_PASS : (a + 1) * K_PASS, :].rearrange("(p i) n -> p i n", i=PACK)
+            )
+            return raw
+
+        tab_w = tile("tab_w", [P, T], I32)
+        nc.sync.dma_start(tab_w[:], tab_words[0].rearrange("p t b -> p (t b)").bitcast(I32))
+        wv_raw = [load_weight("wv", wv, 0)]
+        load_scales(tab_sc, tab_scales)
+        wv_raw.append(load_weight("wv", wv, 1))
+        wkd_raw = [load_weight("wkd", wkd, a) for a in range(PASSES)]
+        wk4_w = tile("wk4_w", [P, PASSES, 2 * N // 4], I32)
+        nc.sync.dma_start(wk4_w[:], wk4_words.bitcast(I32).rearrange("a p c -> p a c"))
+        rec = [tile("rec%d" % h, [P, T], F32) for h in range(HALVES)]
+        for h in range(HALVES):
+            nc.sync.dma_start(rec[h][:], rT[h * P : (h + 1) * P, :])
+        st_sb = tile("st_sb", [P, HALVES, J], F32)
+        nc.sync.dma_start(st_sb[:], st.rearrange("(h p) j -> p h j", p=P))
+        wk4_sc = tile("wk4_sc", [P, PASSES, N // 4], I32)
+        nc.gpsimd.memset(wk4_sc[:], 0)
+        load_scales(wk4_sc, wk4_scales)
 
         def interleaved(grouped):
             return grouped.rearrange("p (c u t) -> p c t u", u=4, t=PACK)
@@ -97,27 +97,15 @@ def tile_list_engram_dl_tier_addL_kernel(
         def planes(raw):
             return raw.rearrange("p t (c u) -> p c t u", u=4)
 
-        def cast(name, raw):
-            grouped = tile(name, [P, PASSES, PACK * N], BF16)
+        def cast(grouped, raw):
             for a in range(PASSES):
                 nc.scalar.copy(interleaved(grouped[:, a, :]), planes(raw[a][:]))
-            return grouped
 
-        def quantise(name, grouped):
-            words = tile(name + "_w", [P, PASSES * N], U32)
-            scales = tile(name + "_sc", [P, PASSES * N], U8)
-            nc.vector.quantize_mx(words[:].bitcast(FP8X4), scales[:], grouped[:].rearrange("p a c -> p (a c)"))
-            return words, scales
+        wv_bf = tile("wv_bf", [P, PASSES, PACK * N], BF16)
+        cast(wv_bf, wv_raw)
+        wkd_bf = tile("wkd_bf", [P, PASSES, PACK * N], BF16)
+        cast(wkd_bf, wkd_raw)
 
-        wv_bf = cast("wv_bf", wv_raw)
-        wkd_bf = cast("wkd_bf", wkd_raw)
-
-        got_w = tile("got_w", [P, J], I32)
-        nc.vector.tensor_copy(got_w[:].bitcast(U32), tab_w[:].bitcast(U32).indirect(offsets[:]))
-        v_w = tile("v_w", [P, PASSES, 2 * J], U8)
-        nc.vector.tensor_copy(
-            v_w[:].bitcast(U16), got_w[:].bitcast(U16).rearrange("p (j d) -> p d j", d=PASSES)
-        )
         v_sc = [tile("v_sc%d" % a, [P, J], U8) for a in range(PASSES)]
 
         def gather_scales(a):
@@ -136,19 +124,23 @@ def tile_list_engram_dl_tier_addL_kernel(
         def columns(a, h):
             return slice(a * N + h * P, a * N + (h + 1) * P)
 
-        def fp8_passes(acc, w, order, first, last):
+        def fp8_passes(acc, w, a, start, stop):
             for h in range(HALVES):
-                for a in order:
-                    cols = columns(a, h)
-                    table_pass(acc[h], w[0][:, cols].bitcast(FP8X4), w[1][:, cols], a,
-                               first and a == order[0], last and a == order[-1])
+                cols = columns(a, h)
+                table_pass(acc[h], w[0][:, cols].bitcast(FP8X4), w[1][:, cols], a, start, stop)
 
-        wq = (tile("wq_w", [P, PASSES * N], U32), tile("wq_sc", [P, PASSES * N], U8))
+        def operand(name):
+            return tile(name + "_w", [P, PASSES * N], U32), tile(name + "_sc", [P, PASSES * N], U8)
+
+        def quantise(w, grouped, a):
+            cols = slice(a * N, (a + 1) * N)
+            nc.vector.quantize_mx(w[0][:, cols].bitcast(FP8X4), w[1][:, cols], grouped[:, a, :])
+
+        wq, wd, wr = operand("wq"), operand("wd"), operand("wr")
         back = {}
 
         def first_tier(a):
-            cols = slice(a * N, (a + 1) * N)
-            nc.vector.quantize_mx(wq[0][:, cols].bitcast(FP8X4), wq[1][:, cols], wv_bf[:, a, :])
+            quantise(wq, wv_bf, a)
             for h in range(HALVES):
                 cols = columns(a, h)
                 bank = ps.tile([P, PACK, P], F32, name="back%d%d" % (a, h))
@@ -161,50 +153,64 @@ def tile_list_engram_dl_tier_addL_kernel(
                     )
                 back[a, h] = bank
 
-        left = tile("left", [P, PASSES, PACK * N], BF16)
+        def leftover(a, h):
+            nc.vector.tensor_tensor(
+                interleaved(left[:, a, h * K_PASS : (h + 1) * K_PASS]),
+                planes(wv_raw[a][:, :, h * P : (h + 1) * P]), planes(back[a, h][:]),
+                ALU.subtract,
+            )
 
-        def leftover(a):
-            for h in range(HALVES):
-                nc.vector.tensor_tensor(
-                    interleaved(left[:, a, h * K_PASS : (h + 1) * K_PASS]),
-                    planes(wv_raw[a][:, :, h * P : (h + 1) * P]), planes(back[a, h][:]),
-                    ALU.subtract,
-                )
-
+        got_w = tile("got_w", [P, J], I32)
+        nc.vector.tensor_copy(got_w[:].bitcast(U32), tab_w[:].bitcast(U32).indirect(offsets[:]))
+        pick_w = tile("pick_w", [P, PACK * P], U32)
+        pick_sc = tile("pick_sc", [P, PACK * P], U8)
+        nc.vector.quantize_mx(pick_w[:].bitcast(FP8X4), pick_sc[:], pick_in[:, 0 : PACK * K_PASS])
+        v_w = tile("v_w", [P, PASSES, 2 * J], U8)
+        nc.vector.tensor_copy(
+            v_w[:].bitcast(U16), got_w[:].bitcast(U16).rearrange("p (j d) -> p d j", d=PASSES)
+        )
         first_tier(0)
         gather_scales(0)
-        first_tier(1)
-        leftover(0)
         gather_scales(1)
-        leftover(1)
+        first_tier(1)
+        for a in range(PASSES):
+            fp8_passes(ve, wq, a, a == 0, False)
+        left = tile("left", [P, PASSES, PACK * N], BF16, "wv_bf")
+        leftover(0, 0)
+        leftover(0, 1)
+        quantise(wd, wkd_bf, 0)
+        fp8_passes(ke, wd, 0, True, False)
+        leftover(1, 0)
+        quantise(wr, left, 0)
+        fp8_passes(ve, wr, 0, False, False)
+        leftover(1, 1)
+        quantise(wd, wkd_bf, 1)
+        fp8_passes(ke, wd, 1, False, False)
         for h in range(HALVES):
             for a in range(PASSES):
                 table_pass(
                     ke[h],
                     wk4_w[:, a, 64 * h : 64 * (h + 1)].bitcast(FP4X4),
                     wk4_sc[:, a, 32 * h : 32 * (h + 1)].bitcast(U8),
-                    a, a == 0, False,
+                    a, False, a == PASSES - 1,
                 )
-        wd = quantise("wd", wkd_bf)
-        fp8_passes(ke, wd, (0, 1), False, True)
-        fp8_passes(ve, wq, (0, 1), True, False)
-        wr = quantise("wr", left)
-        fp8_passes(ve, wr, (0, 1), False, True)
+        quantise(wr, left, 1)
+        fp8_passes(ve, wr, 1, False, True)
 
-        got_rec = [tile("got_rec%d" % h, [P, J], F32) for h in range(HALVES)]
-        gate = [tile("gate%d" % h, [P, J], F32) for h in range(HALVES)]
-        nc.vector.tensor_copy(got_rec[0][:], rec[0][:].indirect(offsets[:]))
+        got_rec = [tile("got_rec0", [P, J], F32, "wv_raw1"), tile("got_rec1", [P, J], F32, "wv_bf")]
         for h in range(HALVES):
-            pre = tile("pre%d" % h, [P, J], F32)
-            nc.vector.tensor_tensor(pre[:], ke[h][:], st_sb[:, h, :], ALU.add)
-            nc.scalar.activation(gate[h][:], pre[:], ACT.Sigmoid)
-        nc.vector.tensor_copy(got_rec[1][:], rec[1][:].indirect(offsets[:]))
-        passed = []
-        for h in range(HALVES):
-            pt = tile("passed%d" % h, [P, J], F32)
-            nc.vector.tensor_tensor(pt[:], ve[h][:], gate[h][:], ALU.mult)
-            passed.append(pt)
-        for h, lo, hi in ((0, 0, J), (1, 0, J // 2), (1, J // 2, J)):
+            nc.vector.tensor_copy(got_rec[h][:], rec[h][:].indirect(offsets[:]))
+        first_fine = ((0, 0, J // 2), (0, J // 2, J), (1, 0, J))
+        last_fine = ((0, 0, J), (1, 0, J // 2), (1, J // 2, J))
+        pre = tile("pre", [P, HALVES, J], F32)
+        gate = tile("gate", [P, HALVES, J], F32)
+        for h, lo, hi in first_fine:
+            nc.vector.tensor_tensor(pre[:, h, lo:hi], ke[h][:, lo:hi], st_sb[:, h, lo:hi], ALU.add)
+            nc.scalar.activation(gate[:, h, lo:hi], pre[:, h, lo:hi], ACT.Sigmoid)
+        passed = tile("passed", [P, HALVES, J], F32)
+        for h, lo, hi in first_fine:
+            nc.vector.tensor_tensor(passed[:, h, lo:hi], ve[h][:, lo:hi], gate[:, h, lo:hi], ALU.mult)
+        for h, lo, hi in last_fine:
             res = tile("res%d_%d" % (h, lo), [P, hi - lo], F32)
-            nc.vector.tensor_tensor(res[:], passed[h][:, lo:hi], got_rec[h][:, lo:hi], ALU.add)
+            nc.vector.tensor_tensor(res[:], passed[:, h, lo:hi], got_rec[h][:, lo:hi], ALU.add)
             nc.sync.dma_start(out[h * P : (h + 1) * P, lo:hi], res[:])

@@ -57,14 +57,13 @@ def tile_list_engram_dl_tier_addL_kernel(
         nc.vector.transpose(own[:], count[:])
         nc.vector.tensor_tensor(eye[:], count[:], own[:], ALU.is_equal)
 
-        warm = tile("warm", [P, 1], F32)
-        nc.scalar.activation(warm[:], eye[:, 0:1], ACT.Sigmoid)
         diagonals = pick_in[:].rearrange("p (i r) -> p i r", i=PACK)
         for b in range(4):
             rows = slice(32 * b, 32 * (b + 1))
-            nc.scalar.copy(
+            nc.scalar.activation(
                 diagonals[rows, :, P * b : P * (b + 1) : PACK],
                 eye[rows, :].unsqueeze(1).to_broadcast([32, PACK, 32]),
+                ACT.Copy,
             )
 
         def load_weight(name, w, a):
@@ -85,11 +84,11 @@ def tile_list_engram_dl_tier_addL_kernel(
         rec = [tile("rec%d" % h, [P, T], F32) for h in range(HALVES)]
         for h in range(HALVES):
             nc.sync.dma_start(rec[h][:], rT[h * P : (h + 1) * P, :])
-        st_sb = tile("st_sb", [P, HALVES, J], F32)
-        nc.sync.dma_start(st_sb[:], st.rearrange("(h p) j -> p h j", p=P))
         wk4_sc = tile("wk4_sc", [P, PASSES, N // 4], I32)
         nc.gpsimd.memset(wk4_sc[:], 0)
         load_scales(wk4_sc, wk4_scales)
+        st_sb = tile("st_sb", [P, HALVES, J], F32)
+        nc.sync.dma_start(st_sb[:], st.rearrange("(h p) j -> p h j", p=P))
 
         def interleaved(grouped):
             return grouped.rearrange("p (c u t) -> p c t u", u=4, t=PACK)
@@ -200,17 +199,24 @@ def tile_list_engram_dl_tier_addL_kernel(
         got_rec = [tile("got_rec0", [P, J], F32, "wv_raw1"), tile("got_rec1", [P, J], F32, "wv_bf")]
         for h in range(HALVES):
             nc.vector.tensor_copy(got_rec[h][:], rec[h][:].indirect(offsets[:]))
-        first_fine = ((0, 0, J // 2), (0, J // 2, J), (1, 0, J))
-        last_fine = ((0, 0, J), (1, 0, J // 2), (1, J // 2, J))
+        pieces = [(h, slice(lo, lo + J // 2)) for h in range(HALVES) for lo in (0, J // 2)]
         pre = tile("pre", [P, HALVES, J], F32)
         gate = tile("gate", [P, HALVES, J], F32)
-        for h, lo, hi in first_fine:
-            nc.vector.tensor_tensor(pre[:, h, lo:hi], ke[h][:, lo:hi], st_sb[:, h, lo:hi], ALU.add)
-            nc.scalar.activation(gate[:, h, lo:hi], pre[:, h, lo:hi], ACT.Sigmoid)
         passed = tile("passed", [P, HALVES, J], F32)
-        for h, lo, hi in first_fine:
-            nc.vector.tensor_tensor(passed[:, h, lo:hi], ve[h][:, lo:hi], gate[:, h, lo:hi], ALU.mult)
-        for h, lo, hi in last_fine:
-            res = tile("res%d_%d" % (h, lo), [P, hi - lo], F32)
-            nc.vector.tensor_tensor(res[:], passed[:, h, lo:hi], got_rec[h][:, lo:hi], ALU.add)
-            nc.sync.dma_start(out[h * P : (h + 1) * P, lo:hi], res[:])
+        result = tile("result", [P, HALVES, J], F32)
+        for h, cols in pieces:
+            nc.vector.tensor_tensor(pre[:, h, cols], ke[h][:, cols], st_sb[:, h, cols], ALU.add)
+            nc.scalar.activation(gate[:, h, cols], pre[:, h, cols], ACT.Sigmoid)
+
+        def let_through(h, cols):
+            nc.vector.tensor_tensor(passed[:, h, cols], ve[h][:, cols], gate[:, h, cols], ALU.mult)
+
+        def finish(h, cols):
+            nc.vector.tensor_tensor(result[:, h, cols], passed[:, h, cols], got_rec[h][:, cols], ALU.add)
+            nc.sync.dma_start(out[h * P : (h + 1) * P, cols], result[:, h, cols])
+
+        let_through(*pieces[0])
+        for ahead, behind in zip(pieces[1:], pieces):
+            let_through(*ahead)
+            finish(*behind)
+        finish(*pieces[-1])

@@ -43,28 +43,29 @@ def tile_list_engram_dl_tier_addL_kernel(
 
         offsets = sb.tile([P, J // 16], U16, name="offsets")
         nc.sync.dma_start(offsets[:], offs)
-        tab_sc = tile("tab_sc", [P, PASSES, T // 4], I32)
+        tab_sc = tile("tab_sc", [P, T // 4], I32)
         nc.gpsimd.memset(tab_sc[:], 0)
 
-        eye = tile("eye", [P, 32], F32)
         ones = tile("ones", [P, 32], F32)
         nc.vector.memset(ones[:], 1.0)
         count = tile("count", [P, 32], F32)
         nc.vector.tensor_tensor_scan(count[:], ones[:], ones[:], 0.0, ALU.mult, ALU.add)
         pick_in = tile("pick_in", [P, PACK * (K_PASS + 1)], BF16)
-        nc.vector.memset(pick_in[:].bitcast(I32), 0)
+        nc.gpsimd.memset(pick_in[:].bitcast(I32), 0)
         own = tile("own", [P, 32], F32)
         nc.vector.transpose(own[:], count[:])
-        nc.vector.tensor_tensor(eye[:], count[:], own[:], ALU.is_equal)
 
         diagonals = pick_in[:].rearrange("p (i r) -> p i r", i=PACK)
         for b in range(4):
             rows = slice(32 * b, 32 * (b + 1))
-            nc.scalar.activation(
+            nc.vector.tensor_scalar(
                 diagonals[rows, :, P * b : P * (b + 1) : PACK],
-                eye[rows, :].unsqueeze(1).to_broadcast([32, PACK, 32]),
-                ACT.Copy,
+                count[rows, :].unsqueeze(1).to_broadcast([32, PACK, 32]),
+                own[rows, 0:1], None, ALU.is_equal,
             )
+        pick_w = tile("pick_w", [P, PACK * P], U32)
+        pick_sc = tile("pick_sc", [P, PACK * P], U8)
+        nc.vector.quantize_mx(pick_w[:].bitcast(FP8X4), pick_sc[:], pick_in[:, 0 : PACK * K_PASS])
 
         def load_weight(name, w, a):
             raw = tile("%s_raw%d" % (name, a), [P, PACK, N], F32)
@@ -73,21 +74,32 @@ def tile_list_engram_dl_tier_addL_kernel(
             )
             return raw
 
+        wv_raw = [load_weight("wv", wv, 0)]
+        for r in range(4):
+            nc.sync.dma_start(
+                tab_sc[r:P:16, :], tab_scales.bitcast(I32)[:, r:16:4, :].rearrange("a q c -> q a c")
+            )
         tab_w = tile("tab_w", [P, T], I32)
         nc.sync.dma_start(tab_w[:], tab_words[0].rearrange("p t b -> p (t b)").bitcast(I32))
-        wv_raw = [load_weight("wv", wv, 0)]
-        load_scales(tab_sc, tab_scales)
         wv_raw.append(load_weight("wv", wv, 1))
-        wkd_raw = [load_weight("wkd", wkd, a) for a in range(PASSES)]
+        wkd_raw = [load_weight("wkd", wkd, 0)]
         wk4_w = tile("wk4_w", [P, PASSES, 2 * N // 4], I32)
         nc.sync.dma_start(wk4_w[:], wk4_words.bitcast(I32).rearrange("a p c -> p a c"))
-        rec = [tile("rec%d" % h, [P, T], F32) for h in range(HALVES)]
-        for h in range(HALVES):
-            nc.sync.dma_start(rec[h][:], rT[h * P : (h + 1) * P, :])
         wk4_sc = tile("wk4_sc", [P, PASSES, N // 4], I32)
+        v_sc = [tile("v_sc%d" % a, [P, J], U8) for a in range(PASSES)]
         nc.gpsimd.memset(wk4_sc[:], 0)
+        nc.gpsimd.memset(v_sc[1][:].bitcast(I32), 0)
         load_scales(wk4_sc, wk4_scales)
-        st_sb = tile("st_sb", [P, HALVES, J], F32)
+
+        nc.vector.tensor_copy(v_sc[0][:], tab_sc[:].bitcast(U8).indirect(offsets[:]))
+        nc.sync.dma_start(v_sc[1][0 : P - 16, :].bitcast(I32), v_sc[0][16:P, :].bitcast(I32))
+        got_w = tile("got_w", [P, J], I32)
+        nc.vector.tensor_copy(got_w[:].bitcast(U32), tab_w[:].bitcast(U32).indirect(offsets[:]))
+
+        wkd_raw.append(load_weight("wkd", wkd, 1))
+        rec = [tile("rec0", [P, T], F32, "tab_sc"), None]
+        nc.sync.dma_start(rec[0][:], rT[0:P, :])
+        st_sb = tile("st_sb", [P, HALVES, J], F32, "tab_w")
         nc.sync.dma_start(st_sb[:], st.rearrange("(h p) j -> p h j", p=P))
 
         def interleaved(grouped):
@@ -104,11 +116,6 @@ def tile_list_engram_dl_tier_addL_kernel(
         cast(wv_bf, wv_raw)
         wkd_bf = tile("wkd_bf", [P, PASSES, PACK * N], BF16)
         cast(wkd_bf, wkd_raw)
-
-        v_sc = [tile("v_sc%d" % a, [P, J], U8) for a in range(PASSES)]
-
-        def gather_scales(a):
-            nc.vector.tensor_copy(v_sc[a][:], tab_sc[:, a, :].bitcast(U8).indirect(offsets[:]))
 
         ke = [ps.tile([P, J], F32, name="ke%d" % h) for h in range(HALVES)]
         ve = [ps.tile([P, J], F32, name="ve%d" % h) for h in range(HALVES)]
@@ -159,48 +166,46 @@ def tile_list_engram_dl_tier_addL_kernel(
                 ALU.subtract,
             )
 
-        got_w = tile("got_w", [P, J], I32)
-        nc.vector.tensor_copy(got_w[:].bitcast(U32), tab_w[:].bitcast(U32).indirect(offsets[:]))
-        pick_w = tile("pick_w", [P, PACK * P], U32)
-        pick_sc = tile("pick_sc", [P, PACK * P], U8)
-        nc.vector.quantize_mx(pick_w[:].bitcast(FP8X4), pick_sc[:], pick_in[:, 0 : PACK * K_PASS])
+        got_rec = [tile("got_rec%d" % h, [P, J], F32) for h in range(HALVES)]
+
+        def gather_record(h):
+            nc.vector.tensor_copy(got_rec[h][:], rec[h][:].indirect(offsets[:]))
+
+        first_tier(0)
         v_w = tile("v_w", [P, PASSES, 2 * J], U8)
         nc.vector.tensor_copy(
             v_w[:].bitcast(U16), got_w[:].bitcast(U16).rearrange("p (j d) -> p d j", d=PASSES)
         )
-        first_tier(0)
-        gather_scales(0)
-        gather_scales(1)
+        rec[1] = tile("rec1", [P, T], F32, "got_w")
+        nc.sync.dma_start(rec[1][:], rT[P : 2 * P, :])
         first_tier(1)
+        left = tile("left", [P, PASSES, PACK * N], BF16, "wv_bf")
+        for a in range(PASSES):
+            for h in range(HALVES):
+                leftover(a, h)
         for a in range(PASSES):
             fp8_passes(ve, wq, a, a == 0, False)
-        left = tile("left", [P, PASSES, PACK * N], BF16, "wv_bf")
-        leftover(0, 0)
-        leftover(0, 1)
-        quantise(wd, wkd_bf, 0)
-        fp8_passes(ke, wd, 0, True, False)
-        leftover(1, 0)
-        quantise(wr, left, 0)
-        fp8_passes(ve, wr, 0, False, False)
-        leftover(1, 1)
-        quantise(wd, wkd_bf, 1)
-        fp8_passes(ke, wd, 1, False, False)
         for h in range(HALVES):
             for a in range(PASSES):
                 table_pass(
                     ke[h],
                     wk4_w[:, a, 64 * h : 64 * (h + 1)].bitcast(FP4X4),
                     wk4_sc[:, a, 32 * h : 32 * (h + 1)].bitcast(U8),
-                    a, False, a == PASSES - 1,
+                    a, a == 0, False,
                 )
+        quantise(wd, wkd_bf, 0)
+        fp8_passes(ke, wd, 0, False, False)
+        quantise(wr, left, 0)
+        fp8_passes(ve, wr, 0, False, False)
+        quantise(wd, wkd_bf, 1)
+        fp8_passes(ke, wd, 1, False, True)
         quantise(wr, left, 1)
         fp8_passes(ve, wr, 1, False, True)
+        gather_record(0)
+        gather_record(1)
 
-        got_rec = [tile("got_rec0", [P, J], F32, "wv_raw1"), tile("got_rec1", [P, J], F32, "wv_bf")]
-        for h in range(HALVES):
-            nc.vector.tensor_copy(got_rec[h][:], rec[h][:].indirect(offsets[:]))
         pieces = [(h, slice(lo, lo + J // 2)) for h in range(HALVES) for lo in (0, J // 2)]
-        pre = tile("pre", [P, HALVES, J], F32)
+        pre = tile("pre", [P, HALVES, J], F32, "got_w")
         gate = tile("gate", [P, HALVES, J], F32)
         passed = tile("passed", [P, HALVES, J], F32)
         result = tile("result", [P, HALVES, J], F32)

@@ -102,11 +102,11 @@ def tile_list_engram_dl_tier_addL_kernel(
         st_sb = tile("st_sb", [P, HALVES, J], F32, "tab_w")
         nc.sync.dma_start(st_sb[:], st.rearrange("(h p) j -> p h j", p=P))
 
-        def interleaved(grouped):
-            return grouped.rearrange("p (c u t) -> p c t u", u=4, t=PACK)
+        def interleaved(grouped, run=4):
+            return grouped.rearrange("p (c u t) -> p c t u", u=run, t=PACK)
 
-        def planes(raw):
-            return raw.rearrange("p t (c u) -> p c t u", u=4)
+        def planes(raw, run=4):
+            return raw.rearrange("p t (c u) -> p c t u", u=run)
 
         def cast(grouped, raw):
             for a in range(PASSES):
@@ -161,8 +161,8 @@ def tile_list_engram_dl_tier_addL_kernel(
 
         def leftover(a, h):
             nc.vector.tensor_tensor(
-                interleaved(left[:, a, h * K_PASS : (h + 1) * K_PASS]),
-                planes(wv_raw[a][:, :, h * P : (h + 1) * P]), planes(back[a, h][:]),
+                interleaved(left[:, a, h * K_PASS : (h + 1) * K_PASS], 2),
+                planes(wv_raw[a][:, :, h * P : (h + 1) * P], 2), planes(back[a, h][:], 2),
                 ALU.subtract,
             )
 

@@ -48,24 +48,32 @@ def tile_list_engram_dl_tier_addL_kernel(
 
         ones = tile("ones", [P, 32], F32)
         nc.vector.memset(ones[:], 1.0)
+        pick_in = tile("pick_in", [P, 2 * (K_PASS + 1)], BF16)
+        nc.vector.memset(pick_in[:].bitcast(I32), 0)
         count = tile("count", [P, 32], F32)
         nc.vector.tensor_tensor_scan(count[:], ones[:], ones[:], 0.0, ALU.mult, ALU.add)
-        pick_in = tile("pick_in", [P, PACK * (K_PASS + 1)], BF16)
-        nc.gpsimd.memset(pick_in[:].bitcast(I32), 0)
+        wk4_sc = tile("wk4_sc", [P, PASSES, N // 4], I32)
+        v_sc = [tile("v_sc%d" % a, [P, J], U8) for a in range(PASSES)]
+        nc.vector.memset(wk4_sc[:], 0)
         own = tile("own", [P, 32], F32)
         nc.vector.transpose(own[:], count[:])
+        nc.vector.memset(v_sc[1][:].bitcast(I32), 0)
 
-        diagonals = pick_in[:].rearrange("p (i r) -> p i r", i=PACK)
+        diagonals = pick_in[:].rearrange("p (i r) -> p i r", i=2)
         for b in range(4):
             rows = slice(32 * b, 32 * (b + 1))
             nc.vector.tensor_scalar(
                 diagonals[rows, :, P * b : P * (b + 1) : PACK],
-                count[rows, :].unsqueeze(1).to_broadcast([32, PACK, 32]),
+                count[rows, :].unsqueeze(1).to_broadcast([32, 2, 32]),
                 own[rows, 0:1], None, ALU.is_equal,
             )
-        pick_w = tile("pick_w", [P, PACK * P], U32)
-        pick_sc = tile("pick_sc", [P, PACK * P], U8)
-        nc.vector.quantize_mx(pick_w[:].bitcast(FP8X4), pick_sc[:], pick_in[:, 0 : PACK * K_PASS])
+        pick_w = [tile("pick_w%d" % u, [P, 2 * P], U32) for u in range(2)]
+        pick_sc = tile("pick_sc", [P, 2 * P], U8)
+        nc.vector.quantize_mx(pick_w[0][:].bitcast(FP8X4), pick_sc[:], pick_in[:, 0 : 2 * K_PASS])
+        nc.vector.tensor_copy(
+            pick_w[1][:].bitcast(U16).rearrange("p (w x) -> p w x", x=2),
+            pick_w[0][:].bitcast(U16).rearrange("p (w x) -> p w x", x=2)[:, :, ::-1],
+        )
 
         def load_weight(name, w, a):
             raw = tile("%s_raw%d" % (name, a), [P, PACK, N], F32)
@@ -82,13 +90,9 @@ def tile_list_engram_dl_tier_addL_kernel(
         tab_w = tile("tab_w", [P, T], I32)
         nc.sync.dma_start(tab_w[:], tab_words[0].rearrange("p t b -> p (t b)").bitcast(I32))
         wv_raw.append(load_weight("wv", wv, 1))
-        wkd_raw = [load_weight("wkd", wkd, 0)]
+        wkd_raw = [load_weight("wkd", wkd, a) for a in range(PASSES)]
         wk4_w = tile("wk4_w", [P, PASSES, 2 * N // 4], I32)
         nc.sync.dma_start(wk4_w[:], wk4_words.bitcast(I32).rearrange("a p c -> p a c"))
-        wk4_sc = tile("wk4_sc", [P, PASSES, N // 4], I32)
-        v_sc = [tile("v_sc%d" % a, [P, J], U8) for a in range(PASSES)]
-        nc.gpsimd.memset(wk4_sc[:], 0)
-        nc.gpsimd.memset(v_sc[1][:].bitcast(I32), 0)
         load_scales(wk4_sc, wk4_scales)
 
         nc.vector.tensor_copy(v_sc[0][:], tab_sc[:].bitcast(U8).indirect(offsets[:]))
@@ -96,11 +100,12 @@ def tile_list_engram_dl_tier_addL_kernel(
         got_w = tile("got_w", [P, J], I32)
         nc.vector.tensor_copy(got_w[:].bitcast(U32), tab_w[:].bitcast(U32).indirect(offsets[:]))
 
-        wkd_raw.append(load_weight("wkd", wkd, 1))
-        rec = [tile("rec0", [P, T], F32, "tab_sc"), None]
+        rec = [tile("rec%d" % h, [P, T], F32) for h in range(HALVES)]
         nc.sync.dma_start(rec[0][:], rT[0:P, :])
-        st_sb = tile("st_sb", [P, HALVES, J], F32, "tab_w")
-        nc.sync.dma_start(st_sb[:], st.rearrange("(h p) j -> p h j", p=P))
+        st_sb = [tile("st_sb%d" % h, [P, J], F32) for h in range(HALVES)]
+        for h in range(HALVES):
+            nc.sync.dma_start(st_sb[h][:], st[h * P : (h + 1) * P, :])
+        nc.sync.dma_start(rec[1][:], rT[P : 2 * P, :])
 
         def interleaved(grouped, run=4):
             return grouped.rearrange("p (c u t) -> p c t u", u=run, t=PACK)
@@ -135,14 +140,14 @@ def tile_list_engram_dl_tier_addL_kernel(
                 cols = columns(a, h)
                 table_pass(acc[h], w[0][:, cols].bitcast(FP8X4), w[1][:, cols], a, start, stop)
 
-        def operand(name):
-            return tile(name + "_w", [P, PASSES * N], U32), tile(name + "_sc", [P, PASSES * N], U8)
+        def operand(name, words_tag=""):
+            return tile(name + "_w", [P, PASSES * N], U32, words_tag), tile(name + "_sc", [P, PASSES * N], U8)
 
         def quantise(w, grouped, a):
             cols = slice(a * N, (a + 1) * N)
             nc.vector.quantize_mx(w[0][:, cols].bitcast(FP8X4), w[1][:, cols], grouped[:, a, :])
 
-        wq, wd, wr = operand("wq"), operand("wd"), operand("wr")
+        wq, wd = operand("wq"), operand("wd")
         back = {}
 
         def first_tier(a):
@@ -151,9 +156,9 @@ def tile_list_engram_dl_tier_addL_kernel(
                 cols = columns(a, h)
                 bank = ps.tile([P, PACK, P], F32, name="back%d%d" % (a, h))
                 for i in range(PACK):
-                    sel = slice(i * P, (i + 1) * P)
+                    sel = slice(i % 2 * P, (i % 2 + 1) * P)
                     nc.tensor.matmul_mx(
-                        bank[:, i, :], lhsT=pick_w[:, sel].bitcast(FP8X4), lhsT_scale=pick_sc[:, sel],
+                        bank[:, i, :], lhsT=pick_w[i // 2][:, sel].bitcast(FP8X4), lhsT_scale=pick_sc[:, sel],
                         rhs=wq[0][:, cols].bitcast(FP8X4), rhs_scale=wq[1][:, cols],
                         start=True, stop=True,
                     )
@@ -166,9 +171,10 @@ def tile_list_engram_dl_tier_addL_kernel(
                 ALU.subtract,
             )
 
-        got_rec = [tile("got_rec%d" % h, [P, J], F32) for h in range(HALVES)]
+        got_rec = []
 
-        def gather_record(h):
+        def gather_record(h, tag):
+            got_rec.append(tile("got_rec%d" % h, [P, J], F32, tag))
             nc.vector.tensor_copy(got_rec[h][:], rec[h][:].indirect(offsets[:]))
 
         first_tier(0)
@@ -176,52 +182,50 @@ def tile_list_engram_dl_tier_addL_kernel(
         nc.vector.tensor_copy(
             v_w[:].bitcast(U16), got_w[:].bitcast(U16).rearrange("p (j d) -> p d j", d=PASSES)
         )
-        rec[1] = tile("rec1", [P, T], F32, "got_w")
-        nc.sync.dma_start(rec[1][:], rT[P : 2 * P, :])
         first_tier(1)
         left = tile("left", [P, PASSES, PACK * N], BF16, "wv_bf")
         for a in range(PASSES):
             for h in range(HALVES):
                 leftover(a, h)
         for a in range(PASSES):
-            fp8_passes(ve, wq, a, a == 0, False)
-        for h in range(HALVES):
-            for a in range(PASSES):
+            for h in range(HALVES):
                 table_pass(
                     ke[h],
                     wk4_w[:, a, 64 * h : 64 * (h + 1)].bitcast(FP4X4),
                     wk4_sc[:, a, 32 * h : 32 * (h + 1)].bitcast(U8),
                     a, a == 0, False,
                 )
-        quantise(wd, wkd_bf, 0)
-        fp8_passes(ke, wd, 0, False, False)
-        quantise(wr, left, 0)
-        fp8_passes(ve, wr, 0, False, False)
-        quantise(wd, wkd_bf, 1)
-        fp8_passes(ke, wd, 1, False, True)
-        quantise(wr, left, 1)
-        fp8_passes(ve, wr, 1, False, True)
-        gather_record(0)
-        gather_record(1)
-
-        pieces = [(h, slice(lo, lo + J // 2)) for h in range(HALVES) for lo in (0, J // 2)]
-        pre = tile("pre", [P, HALVES, J], F32, "got_w")
+        for a in range(PASSES):
+            quantise(wd, wkd_bf, a)
+            fp8_passes(ke, wd, a, False, a == PASSES - 1)
+        gather_record(0, "wv_raw1")
+        wr = operand("wr", "wd_w")
+        for a in range(PASSES):
+            quantise(wr, left, a)
+        value_passes = [(wr, 0), (wq, 0), (wq, 1), (wr, 1)]
+        for h in range(HALVES):
+            for n, (w, a) in enumerate(value_passes):
+                cols = columns(a, h)
+                table_pass(
+                    ve[h], w[0][:, cols].bitcast(FP8X4), w[1][:, cols], a,
+                    n == 0, n == len(value_passes) - 1,
+                )
+        pre = tile("pre", [P, HALVES, J], F32)
         gate = tile("gate", [P, HALVES, J], F32)
         passed = tile("passed", [P, HALVES, J], F32)
         result = tile("result", [P, HALVES, J], F32)
+        warm = tile("warm", [P, 1], F32)
+        nc.scalar.activation(warm[:], wkd_bf[:, 1, 0:1], ACT.Sigmoid)
+        ke_sb = tile("ke_sb", [P, J], F32)
+        nc.scalar.copy(ke_sb[:], ke[1][:])
+        nc.gpsimd.tensor_tensor(pre[:, 1, :], ke_sb[:], st_sb[1][:], ALU.add)
+        nc.vector.tensor_tensor(pre[:, 0, :], ke[0][:], st_sb[0][:], ALU.add)
+        for h in range(HALVES):
+            nc.scalar.activation(gate[:, h, :], pre[:, h, :], ACT.Sigmoid)
+        gather_record(1, "wv_bf")
+        for h in range(HALVES):
+            nc.vector.tensor_tensor(passed[:, h, :], ve[h][:], gate[:, h, :], ALU.mult)
+        pieces = [(h, slice(lo, lo + J // 2)) for h in range(HALVES) for lo in (0, J // 2)]
         for h, cols in pieces:
-            nc.vector.tensor_tensor(pre[:, h, cols], ke[h][:, cols], st_sb[:, h, cols], ALU.add)
-            nc.scalar.activation(gate[:, h, cols], pre[:, h, cols], ACT.Sigmoid)
-
-        def let_through(h, cols):
-            nc.vector.tensor_tensor(passed[:, h, cols], ve[h][:, cols], gate[:, h, cols], ALU.mult)
-
-        def finish(h, cols):
             nc.vector.tensor_tensor(result[:, h, cols], passed[:, h, cols], got_rec[h][:, cols], ALU.add)
             nc.sync.dma_start(out[h * P : (h + 1) * P, cols], result[:, h, cols])
-
-        let_through(*pieces[0])
-        for ahead, behind in zip(pieces[1:], pieces):
-            let_through(*ahead)
-            finish(*behind)
-        finish(*pieces[-1])

@@ -17,10 +17,13 @@ ALU = mybir.AluOpType
 ACT = mybir.ActivationFunctionType
 
 P = 128
+QUAD = 32
 PACK = 4
 K_PASS = P * PACK
 PASSES = K // K_PASS
 HALVES = N // P
+SHIFT = 16
+GPSIMD_COLUMNS = 192
 
 
 def tile_list_engram_dl_tier_addL_kernel(
@@ -34,37 +37,30 @@ def tile_list_engram_dl_tier_addL_kernel(
         def tile(name, shape, dtype, tag=""):
             return sb.tile(shape, dtype, name=name, tag=tag or name, align_bytes=64)
 
-        def load_scales(plane, src):
-            for q in range(4):
-                nc.sync.dma_start(
-                    plane[32 * q : 32 * q + 4, :, :],
-                    src.bitcast(I32)[:, 4 * q : 4 * q + 4, :].rearrange("a r c -> r a c"),
-                )
-
         offsets = sb.tile([P, J // 16], U16, name="offsets")
         nc.sync.dma_start(offsets[:], offs)
         tab_sc = tile("tab_sc", [P, T // 4], I32)
         nc.gpsimd.memset(tab_sc[:], 0)
 
-        ones = tile("ones", [P, 32], F32)
+        ones = tile("ones", [P, QUAD], F32)
         nc.vector.memset(ones[:], 1.0)
         pick_in = tile("pick_in", [P, 2 * (K_PASS + 1)], BF16)
         nc.vector.memset(pick_in[:].bitcast(I32), 0)
-        count = tile("count", [P, 32], F32)
+        count = tile("count", [P, QUAD], F32)
         nc.vector.tensor_tensor_scan(count[:], ones[:], ones[:], 0.0, ALU.mult, ALU.add)
         wk4_sc = tile("wk4_sc", [P, PASSES, N // 4], I32)
         v_sc = [tile("v_sc%d" % a, [P, J], U8) for a in range(PASSES)]
         nc.vector.memset(wk4_sc[:], 0)
-        own = tile("own", [P, 32], F32)
+        own = tile("own", [P, QUAD], F32)
         nc.vector.transpose(own[:], count[:])
         nc.vector.memset(v_sc[1][:].bitcast(I32), 0)
 
         diagonals = pick_in[:].rearrange("p (i r) -> p i r", i=2)
-        for b in range(4):
-            rows = slice(32 * b, 32 * (b + 1))
+        for b in range(P // QUAD):
+            rows = slice(QUAD * b, QUAD * (b + 1))
             nc.vector.tensor_scalar(
                 diagonals[rows, :, P * b : P * (b + 1) : PACK],
-                count[rows, :].unsqueeze(1).to_broadcast([32, 2, 32]),
+                count[rows, :].unsqueeze(1).to_broadcast([QUAD, 2, QUAD]),
                 own[rows, 0:1], None, ALU.is_equal,
             )
         pick_w = [tile("pick_w%d" % u, [P, 2 * P], U32) for u in range(2)]
@@ -85,7 +81,7 @@ def tile_list_engram_dl_tier_addL_kernel(
         wv_raw = [load_weight("wv", wv, 0)]
         for r in range(4):
             nc.sync.dma_start(
-                tab_sc[r:P:16, :], tab_scales.bitcast(I32)[:, r:16:4, :].rearrange("a q c -> q a c")
+                tab_sc[r:P:SHIFT, :], tab_scales.bitcast(I32)[:, r:16:4, :].rearrange("a q c -> q a c")
             )
         tab_w = tile("tab_w", [P, T], I32)
         nc.sync.dma_start(tab_w[:], tab_words[0].rearrange("p t b -> p (t b)").bitcast(I32))
@@ -93,37 +89,47 @@ def tile_list_engram_dl_tier_addL_kernel(
         wkd_raw = [load_weight("wkd", wkd, a) for a in range(PASSES)]
         wk4_w = tile("wk4_w", [P, PASSES, 2 * N // 4], I32)
         nc.sync.dma_start(wk4_w[:], wk4_words.bitcast(I32).rearrange("a p c -> p a c"))
-        load_scales(wk4_sc, wk4_scales)
+        for q in range(P // QUAD):
+            nc.sync.dma_start(
+                wk4_sc[QUAD * q : QUAD * q + 4, :, :],
+                wk4_scales.bitcast(I32)[:, 4 * q : 4 * q + 4, :].rearrange("a r c -> r a c"),
+            )
 
         nc.vector.tensor_copy(v_sc[0][:], tab_sc[:].bitcast(U8).indirect(offsets[:]))
-        nc.sync.dma_start(v_sc[1][0 : P - 16, :].bitcast(I32), v_sc[0][16:P, :].bitcast(I32))
+        nc.sync.dma_start(v_sc[1][0 : P - SHIFT, :].bitcast(I32), v_sc[0][SHIFT:P, :].bitcast(I32))
         got_w = tile("got_w", [P, J], I32)
         nc.vector.tensor_copy(got_w[:].bitcast(U32), tab_w[:].bitcast(U32).indirect(offsets[:]))
 
         rec = [tile("rec%d" % h, [P, T], F32) for h in range(HALVES)]
-        nc.sync.dma_start(rec[0][:], rT[0:P, :])
         st_sb = [tile("st_sb%d" % h, [P, J], F32) for h in range(HALVES)]
         for h in range(HALVES):
+            nc.sync.dma_start(rec[h][:], rT[h * P : (h + 1) * P, :])
             nc.sync.dma_start(st_sb[h][:], st[h * P : (h + 1) * P, :])
-        nc.sync.dma_start(rec[1][:], rT[P : 2 * P, :])
 
-        def interleaved(grouped, run=4):
-            return grouped.rearrange("p (c u t) -> p c t u", u=run, t=PACK)
+        def interleaved(grouped, run):
+            return grouped.rearrange("p (c u i) -> p c i u", u=run, i=PACK)
 
-        def planes(raw, run=4):
-            return raw.rearrange("p t (c u) -> p c t u", u=run)
+        def rows_of(raw, run):
+            return raw.rearrange("p i (c u) -> p c i u", u=run)
 
-        def cast(grouped, raw):
+        def round_weight(grouped, raw):
             for a in range(PASSES):
-                nc.scalar.copy(interleaved(grouped[:, a, :]), planes(raw[a][:]))
+                for h in range(HALVES):
+                    nc.scalar.copy(
+                        interleaved(grouped[:, a, h * K_PASS : (h + 1) * K_PASS], 4),
+                        rows_of(raw[a][:, :, h * P : (h + 1) * P], 4),
+                    )
 
         wv_bf = tile("wv_bf", [P, PASSES, PACK * N], BF16)
-        cast(wv_bf, wv_raw)
+        round_weight(wv_bf, wv_raw)
         wkd_bf = tile("wkd_bf", [P, PASSES, PACK * N], BF16)
-        cast(wkd_bf, wkd_raw)
+        round_weight(wkd_bf, wkd_raw)
 
         ke = [ps.tile([P, J], F32, name="ke%d" % h) for h in range(HALVES)]
         ve = [ps.tile([P, J], F32, name="ve%d" % h) for h in range(HALVES)]
+
+        def columns(a, h):
+            return slice(a * N + h * P, a * N + (h + 1) * P)
 
         def table_pass(acc, words, scales, a, start, stop):
             nc.tensor.matmul_mx(
@@ -132,16 +138,12 @@ def tile_list_engram_dl_tier_addL_kernel(
                 start=start, stop=stop,
             )
 
-        def columns(a, h):
-            return slice(a * N + h * P, a * N + (h + 1) * P)
+        def fp8_pass(acc, w, a, h, start, stop):
+            cols = columns(a, h)
+            table_pass(acc, w[0][:, cols].bitcast(FP8X4), w[1][:, cols], a, start, stop)
 
-        def fp8_passes(acc, w, a, start, stop):
-            for h in range(HALVES):
-                cols = columns(a, h)
-                table_pass(acc[h], w[0][:, cols].bitcast(FP8X4), w[1][:, cols], a, start, stop)
-
-        def operand(name, words_tag=""):
-            return tile(name + "_w", [P, PASSES * N], U32, words_tag), tile(name + "_sc", [P, PASSES * N], U8)
+        def operand(name):
+            return tile(name + "_w", [P, PASSES * N], U32), tile(name + "_sc", [P, PASSES * N], U8)
 
         def quantise(w, grouped, a):
             cols = slice(a * N, (a + 1) * N)
@@ -164,12 +166,42 @@ def tile_list_engram_dl_tier_addL_kernel(
                     )
                 back[a, h] = bank
 
-        def leftover(a, h):
-            nc.vector.tensor_tensor(
-                interleaved(left[:, a, h * K_PASS : (h + 1) * K_PASS], 2),
-                planes(wv_raw[a][:, :, h * P : (h + 1) * P], 2), planes(back[a, h][:], 2),
-                ALU.subtract,
-            )
+        first_tier(0)
+        v_w = tile("v_w", [P, PASSES, 2 * J], U8)
+        nc.vector.tensor_copy(
+            v_w[:].bitcast(U16), got_w[:].bitcast(U16).rearrange("p (j d) -> p d j", d=PASSES)
+        )
+        first_tier(1)
+
+        left = tile("left", [P, PASSES, PACK * N], BF16, "wv_bf")
+        for a in range(PASSES):
+            for h in range(HALVES):
+                nc.vector.tensor_tensor(
+                    interleaved(left[:, a, h * K_PASS : (h + 1) * K_PASS], 2),
+                    rows_of(wv_raw[a][:, :, h * P : (h + 1) * P], 2), rows_of(back[a, h][:], 2),
+                    ALU.subtract,
+                )
+
+        for a in range(PASSES):
+            for h in range(HALVES):
+                table_pass(
+                    ke[h],
+                    wk4_w[:, a, P // 2 * h : P // 2 * (h + 1)].bitcast(FP4X4),
+                    wk4_sc[:, a, P // 4 * h : P // 4 * (h + 1)].bitcast(U8),
+                    a, a == 0, False,
+                )
+        for a in range(PASSES):
+            quantise(wd, wkd_bf, a)
+            for h in (1, 0):
+                fp8_pass(ke[h], wd, a, h, False, a == PASSES - 1)
+
+        wr = operand("wr")
+        for a in range(PASSES):
+            quantise(wr, left, a)
+        value_passes = [(wq, 1), (wq, 0), (wr, 0), (wr, 1)]
+        for h in range(HALVES):
+            for n, (w, a) in enumerate(value_passes):
+                fp8_pass(ve[h], w, a, h, n == 0, n == len(value_passes) - 1)
 
         got_rec = []
 
@@ -177,39 +209,7 @@ def tile_list_engram_dl_tier_addL_kernel(
             got_rec.append(tile("got_rec%d" % h, [P, J], F32, tag))
             nc.vector.tensor_copy(got_rec[h][:], rec[h][:].indirect(offsets[:]))
 
-        first_tier(0)
-        v_w = tile("v_w", [P, PASSES, 2 * J], U8)
-        nc.vector.tensor_copy(
-            v_w[:].bitcast(U16), got_w[:].bitcast(U16).rearrange("p (j d) -> p d j", d=PASSES)
-        )
-        first_tier(1)
-        left = tile("left", [P, PASSES, PACK * N], BF16, "wv_bf")
-        for a in range(PASSES):
-            for h in range(HALVES):
-                leftover(a, h)
-        for a in range(PASSES):
-            for h in range(HALVES):
-                table_pass(
-                    ke[h],
-                    wk4_w[:, a, 64 * h : 64 * (h + 1)].bitcast(FP4X4),
-                    wk4_sc[:, a, 32 * h : 32 * (h + 1)].bitcast(U8),
-                    a, a == 0, False,
-                )
-        for a in range(PASSES):
-            quantise(wd, wkd_bf, a)
-            fp8_passes(ke, wd, a, False, a == PASSES - 1)
         gather_record(0, "wv_raw1")
-        wr = operand("wr", "wd_w")
-        for a in range(PASSES):
-            quantise(wr, left, a)
-        value_passes = [(wr, 0), (wq, 0), (wq, 1), (wr, 1)]
-        for h in range(HALVES):
-            for n, (w, a) in enumerate(value_passes):
-                cols = columns(a, h)
-                table_pass(
-                    ve[h], w[0][:, cols].bitcast(FP8X4), w[1][:, cols], a,
-                    n == 0, n == len(value_passes) - 1,
-                )
         pre = tile("pre", [P, HALVES, J], F32)
         gate = tile("gate", [P, HALVES, J], F32)
         passed = tile("passed", [P, HALVES, J], F32)
@@ -225,7 +225,10 @@ def tile_list_engram_dl_tier_addL_kernel(
         gather_record(1, "wv_bf")
         for h in range(HALVES):
             nc.vector.tensor_tensor(passed[:, h, :], ve[h][:], gate[:, h, :], ALU.mult)
-        pieces = [(h, slice(lo, lo + J // 2)) for h in range(HALVES) for lo in (0, J // 2)]
-        for h, cols in pieces:
-            nc.vector.tensor_tensor(result[:, h, cols], passed[:, h, cols], got_rec[h][:, cols], ALU.add)
+        pieces = [
+            (nc.gpsimd, 0, slice(0, GPSIMD_COLUMNS)), (nc.vector, 0, slice(GPSIMD_COLUMNS, J)),
+            (nc.vector, 1, slice(0, J // 2)), (nc.vector, 1, slice(J // 2, J)),
+        ]
+        for engine, h, cols in pieces:
+            engine.tensor_tensor(result[:, h, cols], passed[:, h, cols], got_rec[h][:, cols], ALU.add)
             nc.sync.dma_start(out[h * P : (h + 1) * P, cols], result[:, h, cols])

@@ -116,8 +116,8 @@ def tile_list_engram_dl_tier_addL_kernel(
             for a in range(PASSES):
                 for h in range(HALVES):
                     nc.scalar.copy(
-                        interleaved(grouped[:, a, h * K_PASS : (h + 1) * K_PASS], 4),
-                        rows_of(raw[a][:, :, h * P : (h + 1) * P], 4),
+                        interleaved(grouped[:, a, h * K_PASS : (h + 1) * K_PASS], 2),
+                        rows_of(raw[a][:, :, h * P : (h + 1) * P], 2),
                     )
 
         wv_bf = tile("wv_bf", [P, PASSES, PACK * N], BF16)

@@ -33,6 +33,10 @@ def tile_list_engram_dl_tier_addL_kernel(
     with ExitStack() as ctx:
         sb = ctx.enter_context(tc.tile_pool(name="sb", bufs=1))
         ps = ctx.enter_context(tc.psum_pool(name="ps", bufs=1))
+        shared = ctx.enter_context(tc.tile_pool(name="shared", bufs=1))
+
+        def placed(name, shape, dtype, offset):
+            return shared.tile(shape, dtype, name=name, offset=offset, align_bytes=64)
 
         def tile(name, shape, dtype, tag=""):
             return sb.tile(shape, dtype, name=name, tag=tag or name, align_bytes=64)
@@ -97,14 +101,25 @@ def tile_list_engram_dl_tier_addL_kernel(
 
         nc.vector.tensor_copy(v_sc[0][:], tab_sc[:].bitcast(U8).indirect(offsets[:]))
         nc.sync.dma_start(v_sc[1][0 : P - SHIFT, :].bitcast(I32), v_sc[0][SHIFT:P, :].bitcast(I32))
-        got_w = tile("got_w", [P, J], I32)
-        nc.vector.tensor_copy(got_w[:].bitcast(U32), tab_w[:].bitcast(U32).indirect(offsets[:]))
+        ke = [ps.tile([P, J], F32, name="ke%d" % h) for h in range(HALVES)]
+        ve = [ps.tile([P, J], F32, name="ve%d" % h) for h in range(HALVES)]
+        for u in range(3):
+            nc.tensor.matmul_mx(
+                ve[1][:, 0 : 2 * P], lhsT=pick_w[1][:, 0:P].bitcast(FP8X4), lhsT_scale=pick_sc[:, 0:P],
+                rhs=pick_w[1][:].bitcast(FP8X4), rhs_scale=tab_sc[:].bitcast(U8)[:, 0 : 2 * P], start=True, stop=True,
+            )
+        got_w = [tile("got_w%d" % u, [P, J // 2], I32) for u in range(2)]
+        for u in range(2):
+            nc.vector.tensor_copy(
+                got_w[u][:].bitcast(U32), tab_w[:].bitcast(U32).indirect(offsets[:, 16 * u : 16 * (u + 1)])
+            )
 
         rec = [tile("rec%d" % h, [P, T], F32) for h in range(HALVES)]
         st_sb = [tile("st_sb%d" % h, [P, J], F32) for h in range(HALVES)]
-        for h in range(HALVES):
-            nc.sync.dma_start(rec[h][:], rT[h * P : (h + 1) * P, :])
+        nc.sync.dma_start(rec[1][:], rT[P : 2 * P, :])
+        for h in (1, 0):
             nc.sync.dma_start(st_sb[h][:], st[h * P : (h + 1) * P, :])
+        nc.sync.dma_start(rec[0][:], rT[0:P, :])
 
         def interleaved(grouped, run):
             return grouped.rearrange("p (c u i) -> p c i u", u=run, i=PACK)
@@ -116,17 +131,15 @@ def tile_list_engram_dl_tier_addL_kernel(
             for a in range(PASSES):
                 for h in range(HALVES):
                     nc.scalar.copy(
-                        interleaved(grouped[:, a, h * K_PASS : (h + 1) * K_PASS], 2),
+                        interleaved(grouped[a][h], 2),
                         rows_of(raw[a][:, :, h * P : (h + 1) * P], 2),
                     )
 
-        wv_bf = tile("wv_bf", [P, PASSES, PACK * N], BF16)
-        round_weight(wv_bf, wv_raw)
-        wkd_bf = tile("wkd_bf", [P, PASSES, PACK * N], BF16)
-        round_weight(wkd_bf, wkd_raw)
-
-        ke = [ps.tile([P, J], F32, name="ke%d" % h) for h in range(HALVES)]
-        ve = [ps.tile([P, J], F32, name="ve%d" % h) for h in range(HALVES)]
+        warm = tile("warm", [P, 1], F32)
+        nc.scalar.activation(warm[:], wv_raw[0][:, 0, 0:1], ACT.Sigmoid)
+        wv_bf0 = tile("wv_bf0", [P, PACK * N], BF16)
+        wv_bf1 = [placed("wv_bf10", [P, K_PASS], BF16, 0), tile("wv_bf11", [P, K_PASS], BF16)]
+        round_weight([[wv_bf0[:, 0:K_PASS], wv_bf0[:, K_PASS : 2 * K_PASS]], [t[:] for t in wv_bf1]], wv_raw)
 
         def columns(a, h):
             return slice(a * N + h * P, a * N + (h + 1) * P)
@@ -153,7 +166,11 @@ def tile_list_engram_dl_tier_addL_kernel(
         back = {}
 
         def first_tier(a):
-            quantise(wq, wv_bf, a)
+            if a == 0:
+                nc.vector.quantize_mx(wq[0][:, 0:N].bitcast(FP8X4), wq[1][:, 0:N], wv_bf0[:])
+            else:
+                for h in range(HALVES):
+                    nc.vector.quantize_mx(wq[0][:, columns(a, h)].bitcast(FP8X4), wq[1][:, columns(a, h)], wv_bf1[h][:])
             for h in range(HALVES):
                 cols = columns(a, h)
                 bank = ps.tile([P, PACK, P], F32, name="back%d%d" % (a, h))
@@ -168,19 +185,24 @@ def tile_list_engram_dl_tier_addL_kernel(
 
         first_tier(0)
         v_w = tile("v_w", [P, PASSES, 2 * J], U8)
-        nc.vector.tensor_copy(
-            v_w[:].bitcast(U16), got_w[:].bitcast(U16).rearrange("p (j d) -> p d j", d=PASSES)
-        )
+        for u in range(2):
+            nc.vector.tensor_copy(
+                v_w[:].bitcast(U16)[:, :, u * J // 2 : (u + 1) * J // 2],
+                got_w[u][:].bitcast(U16).rearrange("p (j d) -> p d j", d=PASSES),
+            )
         first_tier(1)
 
-        left = tile("left", [P, PASSES, PACK * N], BF16, "wv_bf")
+        left = placed("left", [P, PASSES, PACK * N], BF16, 0)
+        wkd_bf = tile("wkd_bf", [P, PASSES, PACK * N], BF16)
+        round_weight([[wkd_bf[:, a, h * K_PASS : (h + 1) * K_PASS] for h in range(HALVES)] for a in range(PASSES)], wkd_raw)
         for a in range(PASSES):
-            for h in range(HALVES):
-                nc.vector.tensor_tensor(
-                    interleaved(left[:, a, h * K_PASS : (h + 1) * K_PASS], 2),
-                    rows_of(wv_raw[a][:, :, h * P : (h + 1) * P], 2), rows_of(back[a, h][:], 2),
-                    ALU.subtract,
-                )
+            quantise(wd, wkd_bf, a)
+        for a, h in ((0, 0), (0, 1), (1, 0), (1, 1)):
+            nc.vector.tensor_tensor(
+                interleaved(left[:, a, h * K_PASS : (h + 1) * K_PASS], 2),
+                rows_of(wv_raw[a][:, :, h * P : (h + 1) * P], 2), rows_of(back[a, h][:], 2),
+                ALU.subtract,
+            )
 
         for a in range(PASSES):
             for h in range(HALVES):
@@ -190,45 +212,43 @@ def tile_list_engram_dl_tier_addL_kernel(
                     wk4_sc[:, a, P // 4 * h : P // 4 * (h + 1)].bitcast(U8),
                     a, a == 0, False,
                 )
-        for a in range(PASSES):
-            quantise(wd, wkd_bf, a)
-            for h in (1, 0):
-                fp8_pass(ke[h], wd, a, h, False, a == PASSES - 1)
+        for h in (1, 0):
+            fp8_pass(ke[h], wd, 0, h, False, False)
+        for h in range(HALVES):
+            for a in range(PASSES):
+                fp8_pass(ve[h], wq, a, h, a == 0, False)
+        for h in (1, 0):
+            fp8_pass(ke[h], wd, 1, h, False, True)
 
         wr = operand("wr")
         for a in range(PASSES):
             quantise(wr, left, a)
-        value_passes = [(wq, 1), (wq, 0), (wr, 0), (wr, 1)]
-        for h in range(HALVES):
-            for n, (w, a) in enumerate(value_passes):
-                fp8_pass(ve[h], w, a, h, n == 0, n == len(value_passes) - 1)
+        for h in (1, 0):
+            for a in range(PASSES):
+                fp8_pass(ve[h], wr, a, h, False, a == PASSES - 1)
 
-        got_rec = []
-
-        def gather_record(h, tag):
-            got_rec.append(tile("got_rec%d" % h, [P, J], F32, tag))
-            nc.vector.tensor_copy(got_rec[h][:], rec[h][:].indirect(offsets[:]))
-
-        gather_record(0, "wv_raw1")
         pre = tile("pre", [P, HALVES, J], F32)
         gate = tile("gate", [P, HALVES, J], F32)
         passed = tile("passed", [P, HALVES, J], F32)
         result = tile("result", [P, HALVES, J], F32)
-        warm = tile("warm", [P, 1], F32)
-        nc.scalar.activation(warm[:], wkd_bf[:, 1, 0:1], ACT.Sigmoid)
-        ke_sb = tile("ke_sb", [P, J], F32)
-        nc.scalar.copy(ke_sb[:], ke[1][:])
-        nc.gpsimd.tensor_tensor(pre[:, 1, :], ke_sb[:], st_sb[1][:], ALU.add)
-        nc.vector.tensor_tensor(pre[:, 0, :], ke[0][:], st_sb[0][:], ALU.add)
-        for h in range(HALVES):
-            nc.scalar.activation(gate[:, h, :], pre[:, h, :], ACT.Sigmoid)
-        gather_record(1, "wv_bf")
-        for h in range(HALVES):
-            nc.vector.tensor_tensor(passed[:, h, :], ve[h][:], gate[:, h, :], ALU.mult)
-        pieces = [
-            (nc.gpsimd, 0, slice(0, GPSIMD_COLUMNS)), (nc.vector, 0, slice(GPSIMD_COLUMNS, J)),
-            (nc.vector, 1, slice(0, J // 2)), (nc.vector, 1, slice(J // 2, J)),
-        ]
-        for engine, h, cols in pieces:
-            engine.tensor_tensor(result[:, h, cols], passed[:, h, cols], got_rec[h][:, cols], ALU.add)
-            nc.sync.dma_start(out[h * P : (h + 1) * P, cols], result[:, h, cols])
+        for h, c0, c1 in ((1, 0, 256), (1, 256, J), (0, 0, J)):
+            nc.vector.tensor_tensor(pre[:, h, c0:c1], ke[h][:, c0:c1], st_sb[h][:, c0:c1], ALU.add)
+            nc.scalar.activation(gate[:, h, c0:c1], pre[:, h, c0:c1], ACT.Sigmoid)
+
+        def product(h, c0, c1):
+            nc.vector.tensor_tensor(passed[:, h, c0:c1], ve[h][:, c0:c1], gate[:, h, c0:c1], ALU.mult)
+
+        def finish(h, c0, c1):
+            nc.vector.tensor_tensor(
+                result[:, h, c0:c1], rec[h][:].indirect(offsets[:, c0 // 16 : c1 // 16]), passed[:, h, c0:c1], ALU.add
+            )
+            nc.sync.dma_start(out[h * P : (h + 1) * P, c0:c1], result[:, h, c0:c1])
+
+        product(1, 0, 256)
+        product(1, 256, J)
+        finish(1, 0, 256)
+        finish(1, 256, J)
+        product(0, 0, 320)
+        product(0, 320, J)
+        finish(0, 0, 320)
+        finish(0, 320, J)

@@ -91,7 +91,10 @@ def tile_list_engram_dl_tier_addL_kernel(
         nc.sync.dma_start(tab_w[:], tab_words[0].rearrange("p t b -> p (t b)").bitcast(I32))
         wv_raw.append(load_weight("wv", wv, 1))
         wkd_raw = [load_weight("wkd", wkd, a) for a in range(PASSES)]
-        wk4_w = tile("wk4_w", [P, PASSES, 2 * N // 4], I32)
+
+        nc.vector.tensor_copy(v_sc[0][:], tab_sc[:].bitcast(U8).indirect(offsets[:]))
+        nc.sync.dma_start(v_sc[1][0 : P - SHIFT, :].bitcast(I32), v_sc[0][SHIFT:P, :].bitcast(I32))
+        wk4_w = placed("wk4_w", [P, PASSES, 2 * N // 4], I32, 10240)
         nc.sync.dma_start(wk4_w[:], wk4_words.bitcast(I32).rearrange("a p c -> p a c"))
         for q in range(P // QUAD):
             nc.sync.dma_start(
@@ -99,8 +102,6 @@ def tile_list_engram_dl_tier_addL_kernel(
                 wk4_scales.bitcast(I32)[:, 4 * q : 4 * q + 4, :].rearrange("a r c -> r a c"),
             )
 
-        nc.vector.tensor_copy(v_sc[0][:], tab_sc[:].bitcast(U8).indirect(offsets[:]))
-        nc.sync.dma_start(v_sc[1][0 : P - SHIFT, :].bitcast(I32), v_sc[0][SHIFT:P, :].bitcast(I32))
         ke = [ps.tile([P, J], F32, name="ke%d" % h) for h in range(HALVES)]
         ve = [ps.tile([P, J], F32, name="ve%d" % h) for h in range(HALVES)]
         for u in range(3):
@@ -116,33 +117,22 @@ def tile_list_engram_dl_tier_addL_kernel(
 
         rec = [tile("rec%d" % h, [P, T], F32) for h in range(HALVES)]
         st_sb = [tile("st_sb%d" % h, [P, J], F32) for h in range(HALVES)]
-        nc.sync.dma_start(rec[1][:], rT[P : 2 * P, :])
-        for h in (1, 0):
-            nc.sync.dma_start(st_sb[h][:], st[h * P : (h + 1) * P, :])
         nc.sync.dma_start(rec[0][:], rT[0:P, :])
+        for h in range(HALVES):
+            nc.sync.dma_start(st_sb[h][:], st[h * P : (h + 1) * P, :])
+        nc.sync.dma_start(rec[1][:], rT[P : 2 * P, :])
 
-        def interleaved(grouped, run):
-            return grouped.rearrange("p (c u i) -> p c i u", u=run, i=PACK)
+        def interleaved(grouped):
+            return grouped.rearrange("p (c u i) -> p c i u", u=2, i=PACK)
 
-        def rows_of(raw, run):
-            return raw.rearrange("p i (c u) -> p c i u", u=run)
+        def rows_of(raw):
+            return raw.rearrange("p i (c u) -> p c i u", u=2)
 
-        def round_weight(grouped, raw):
-            for a in range(PASSES):
-                for h in range(HALVES):
-                    nc.scalar.copy(
-                        interleaved(grouped[a][h], 2),
-                        rows_of(raw[a][:, :, h * P : (h + 1) * P], 2),
-                    )
+        def half(raw, h):
+            return raw[:, :, h * P : (h + 1) * P]
 
-        warm = tile("warm", [P, 1], F32)
-        nc.scalar.activation(warm[:], wv_raw[0][:, 0, 0:1], ACT.Sigmoid)
-        wv_bf0 = tile("wv_bf0", [P, PACK * N], BF16)
-        wv_bf1 = [placed("wv_bf10", [P, K_PASS], BF16, 0), tile("wv_bf11", [P, K_PASS], BF16)]
-        round_weight([[wv_bf0[:, 0:K_PASS], wv_bf0[:, K_PASS : 2 * K_PASS]], [t[:] for t in wv_bf1]], wv_raw)
-
-        def columns(a, h):
-            return slice(a * N + h * P, a * N + (h + 1) * P)
+        def round_half(grouped, raw, h):
+            nc.scalar.copy(interleaved(grouped), rows_of(half(raw, h)))
 
         def table_pass(acc, words, scales, a, start, stop):
             nc.tensor.matmul_mx(
@@ -151,92 +141,108 @@ def tile_list_engram_dl_tier_addL_kernel(
                 start=start, stop=stop,
             )
 
-        def fp8_pass(acc, w, a, h, start, stop):
-            cols = columns(a, h)
-            table_pass(acc, w[0][:, cols].bitcast(FP8X4), w[1][:, cols], a, start, stop)
-
         def operand(name):
-            return tile(name + "_w", [P, PASSES * N], U32), tile(name + "_sc", [P, PASSES * N], U8)
+            return tile(name + "_w", [P, 4 * P], U32), tile(name + "_sc", [P, 4 * P], U8)
 
-        def quantise(w, grouped, a):
-            cols = slice(a * N, (a + 1) * N)
-            nc.vector.quantize_mx(w[0][:, cols].bitcast(FP8X4), w[1][:, cols], grouped[:, a, :])
+        def blocks(w, first, count):
+            cols = slice(first * P, (first + count) * P)
+            return w[0][:, cols].bitcast(FP8X4), w[1][:, cols]
+
+        def quantise(w, first, count, grouped):
+            nc.vector.quantize_mx(*blocks(w, first, count), grouped)
+
+        warm = tile("warm", [P, 1], F32)
+        nc.scalar.activation(warm[:], wv_raw[0][:, 0, 0:1], ACT.Sigmoid)
+        wv_bf0 = tile("wv_bf0", [P, HALVES, K_PASS], BF16)
+        wv_bf1 = [placed("wv_bf10", [P, K_PASS], BF16, 0), tile("wv_bf11", [P, K_PASS], BF16)]
+        for h in range(HALVES):
+            round_half(wv_bf0[:, h, :], wv_raw[0], h)
+        for h in range(HALVES):
+            round_half(wv_bf1[h][:], wv_raw[1], h)
 
         wq, wd = operand("wq"), operand("wd")
         back = {}
 
-        def first_tier(a):
-            if a == 0:
-                nc.vector.quantize_mx(wq[0][:, 0:N].bitcast(FP8X4), wq[1][:, 0:N], wv_bf0[:])
-            else:
-                for h in range(HALVES):
-                    nc.vector.quantize_mx(wq[0][:, columns(a, h)].bitcast(FP8X4), wq[1][:, columns(a, h)], wv_bf1[h][:])
-            for h in range(HALVES):
-                cols = columns(a, h)
-                bank = ps.tile([P, PACK, P], F32, name="back%d%d" % (a, h))
-                for i in range(PACK):
-                    sel = slice(i % 2 * P, (i % 2 + 1) * P)
-                    nc.tensor.matmul_mx(
-                        bank[:, i, :], lhsT=pick_w[i // 2][:, sel].bitcast(FP8X4), lhsT_scale=pick_sc[:, sel],
-                        rhs=wq[0][:, cols].bitcast(FP8X4), rhs_scale=wq[1][:, cols],
-                        start=True, stop=True,
-                    )
-                back[a, h] = bank
+        def bring_back(a, h):
+            words, scales = blocks(wq, 2 * a + h, 1)
+            bank = ps.tile([P, PACK, P], F32, name="back%d%d" % (a, h))
+            for i in range(PACK):
+                sel = slice(i % 2 * P, (i % 2 + 1) * P)
+                nc.tensor.matmul_mx(
+                    bank[:, i, :], lhsT=pick_w[i // 2][:, sel].bitcast(FP8X4), lhsT_scale=pick_sc[:, sel],
+                    rhs=words, rhs_scale=scales, start=True, stop=True,
+                )
+            back[a, h] = bank
 
-        first_tier(0)
+        quantise(wq, 0, 2, wv_bf0[:].rearrange("p h c -> p (h c)"))
+        for h in range(HALVES):
+            bring_back(0, h)
         v_w = tile("v_w", [P, PASSES, 2 * J], U8)
         for u in range(2):
             nc.vector.tensor_copy(
                 v_w[:].bitcast(U16)[:, :, u * J // 2 : (u + 1) * J // 2],
                 got_w[u][:].bitcast(U16).rearrange("p (j d) -> p d j", d=PASSES),
             )
-        first_tier(1)
+        for h in range(HALVES):
+            quantise(wq, 2 + h, 1, wv_bf1[h][:])
+            bring_back(1, h)
 
-        left = placed("left", [P, PASSES, PACK * N], BF16, 0)
-        wkd_bf = tile("wkd_bf", [P, PASSES, PACK * N], BF16)
-        round_weight([[wkd_bf[:, a, h * K_PASS : (h + 1) * K_PASS] for h in range(HALVES)] for a in range(PASSES)], wkd_raw)
-        for a in range(PASSES):
-            quantise(wd, wkd_bf, a)
-        for a, h in ((0, 0), (0, 1), (1, 0), (1, 1)):
+        left = placed("left", [P, 3, K_PASS], BF16, 0)
+        wkd_bf0 = placed("wkd_bf0", [P, HALVES, K_PASS], BF16, 4096)
+        wkd_bf1 = [placed("wkd_bf10", [P, K_PASS], BF16, 6144), tile("wkd_bf11", [P, K_PASS], BF16)]
+        for h in range(HALVES):
+            round_half(wkd_bf0[:, h, :], wkd_raw[0], h)
+        for h in range(HALVES):
+            round_half(wkd_bf1[h][:], wkd_raw[1], h)
+        quantise(wd, 0, 2, wkd_bf0[:].rearrange("p a c -> p (a c)"))
+        for h in range(HALVES):
+            quantise(wd, 2 + h, 1, wkd_bf1[h][:])
+        for n, (a, h) in enumerate(((0, 0), (0, 1), (1, 0))):
             nc.vector.tensor_tensor(
-                interleaved(left[:, a, h * K_PASS : (h + 1) * K_PASS], 2),
-                rows_of(wv_raw[a][:, :, h * P : (h + 1) * P], 2), rows_of(back[a, h][:], 2),
-                ALU.subtract,
+                interleaved(left[:, n, :]), rows_of(half(wv_raw[a], h)), rows_of(back[a, h][:]), ALU.subtract
             )
 
         for a in range(PASSES):
-            for h in range(HALVES):
+            table_pass(ve[0], *blocks(wq, 2 * a, 1), a, a == 0, False)
+        for h in range(HALVES):
+            for a in range(PASSES):
                 table_pass(
                     ke[h],
                     wk4_w[:, a, P // 2 * h : P // 2 * (h + 1)].bitcast(FP4X4),
                     wk4_sc[:, a, P // 4 * h : P // 4 * (h + 1)].bitcast(U8),
                     a, a == 0, False,
                 )
-        for h in (1, 0):
-            fp8_pass(ke[h], wd, 0, h, False, False)
         for h in range(HALVES):
             for a in range(PASSES):
-                fp8_pass(ve[h], wq, a, h, a == 0, False)
-        for h in (1, 0):
-            fp8_pass(ke[h], wd, 1, h, False, True)
-
-        wr = operand("wr")
+                table_pass(ke[h], *blocks(wd, 2 * a + h, 1), a, False, a == PASSES - 1)
+        wr = tile("wr_w", [P, 3 * P], U32), placed("wr_sc", [P, 3 * P], U8, 10240)
+        quantise(wr, 0, 2, left[:, 0:2, :].rearrange("p a c -> p (a c)"))
+        quantise(wr, 2, 1, left[:, 2, :])
+        back_sb = placed("back_sb", [P, P, PACK], F32, 4096)
+        left_late = placed("left_late", [P, K_PASS], BF16, 0)
+        nc.scalar.copy(back_sb[:], back[1, 1][:].rearrange("p i c -> p c i"))
+        nc.gpsimd.tensor_tensor(
+            left_late[:].rearrange("p (c i) -> p c i", i=PACK),
+            half(wv_raw[1], 1).rearrange("p i c -> p c i"), back_sb[:], ALU.subtract,
+        )
         for a in range(PASSES):
-            quantise(wr, left, a)
-        for h in (1, 0):
-            for a in range(PASSES):
-                fp8_pass(ve[h], wr, a, h, False, a == PASSES - 1)
+            table_pass(ve[0], *blocks(wr, 2 * a, 1), a, False, a == PASSES - 1)
 
         pre = tile("pre", [P, HALVES, J], F32)
+        gate_first = placed("gate_first", [P, 256], F32, 8192)
         gate = tile("gate", [P, HALVES, J], F32)
         passed = tile("passed", [P, HALVES, J], F32)
         result = tile("result", [P, HALVES, J], F32)
-        for h, c0, c1 in ((1, 0, 256), (1, 256, J), (0, 0, J)):
+
+        def gate_of(h, c0, c1):
+            return gate_first[:] if (h, c0) == (0, 0) else gate[:, h, c0:c1]
+
+        for h, c0, c1 in ((0, 0, 256), (0, 256, J), (1, 0, J)):
             nc.vector.tensor_tensor(pre[:, h, c0:c1], ke[h][:, c0:c1], st_sb[h][:, c0:c1], ALU.add)
-            nc.scalar.activation(gate[:, h, c0:c1], pre[:, h, c0:c1], ACT.Sigmoid)
+            nc.scalar.activation(gate_of(h, c0, c1), pre[:, h, c0:c1], ACT.Sigmoid)
 
         def product(h, c0, c1):
-            nc.vector.tensor_tensor(passed[:, h, c0:c1], ve[h][:, c0:c1], gate[:, h, c0:c1], ALU.mult)
+            nc.vector.tensor_tensor(passed[:, h, c0:c1], ve[h][:, c0:c1], gate_of(h, c0, c1), ALU.mult)
 
         def finish(h, c0, c1):
             nc.vector.tensor_tensor(
@@ -244,11 +250,17 @@ def tile_list_engram_dl_tier_addL_kernel(
             )
             nc.sync.dma_start(out[h * P : (h + 1) * P, c0:c1], result[:, h, c0:c1])
 
-        product(1, 0, 256)
-        product(1, 256, J)
-        finish(1, 0, 256)
-        finish(1, 256, J)
-        product(0, 0, 320)
-        product(0, 320, J)
-        finish(0, 0, 320)
-        finish(0, 320, J)
+        product(0, 0, 256)
+        product(0, 256, J)
+        late = placed("late_w", [P, P], U32, 8192), tile("late_sc", [P, P], U8)
+        quantise(late, 0, 1, left_late[:])
+        table_pass(ve[1], *blocks(wr, 1, 1), 0, True, False)
+        table_pass(ve[1], *blocks(wq, 1, 1), 0, False, False)
+        table_pass(ve[1], *blocks(wq, 3, 1), 1, False, False)
+        table_pass(ve[1], *blocks(late, 0, 1), 1, False, True)
+        finish(0, 0, 256)
+        finish(0, 256, J)
+        product(1, 0, 320)
+        product(1, 320, J)
+        finish(1, 0, 320)
+        finish(1, 320, J)

@@ -104,11 +104,6 @@ def tile_list_engram_dl_tier_addL_kernel(
 
         ke = [ps.tile([P, J], F32, name="ke%d" % h) for h in range(HALVES)]
         ve = [ps.tile([P, J], F32, name="ve%d" % h) for h in range(HALVES)]
-        for u in range(3):
-            nc.tensor.matmul_mx(
-                ve[1][:, 0 : 2 * P], lhsT=pick_w[1][:, 0:P].bitcast(FP8X4), lhsT_scale=pick_sc[:, 0:P],
-                rhs=pick_w[1][:].bitcast(FP8X4), rhs_scale=tab_sc[:].bitcast(U8)[:, 0 : 2 * P], start=True, stop=True,
-            )
         got_w = [tile("got_w%d" % u, [P, J // 2], I32) for u in range(2)]
         for u in range(2):
             nc.vector.tensor_copy(

@@ -22,8 +22,11 @@ PACK = 4
 K_PASS = P * PACK
 PASSES = K // K_PASS
 HALVES = N // P
+PER_COLUMN = 16
 SHIFT = 16
-GPSIMD_COLUMNS = 192
+RUN = 2
+MID = J // 2
+CUT = 320
 
 
 def tile_list_engram_dl_tier_addL_kernel(
@@ -33,16 +36,16 @@ def tile_list_engram_dl_tier_addL_kernel(
     with ExitStack() as ctx:
         sb = ctx.enter_context(tc.tile_pool(name="sb", bufs=1))
         ps = ctx.enter_context(tc.psum_pool(name="ps", bufs=1))
-        shared = ctx.enter_context(tc.tile_pool(name="shared", bufs=1))
-
-        def placed(name, shape, dtype, offset):
-            return shared.tile(shape, dtype, name=name, offset=offset, align_bytes=64)
 
         def tile(name, shape, dtype, tag=""):
             return sb.tile(shape, dtype, name=name, tag=tag or name, align_bytes=64)
 
-        offsets = sb.tile([P, J // 16], U16, name="offsets")
+        offsets = sb.tile([P, J // PER_COLUMN], U16, name="offsets")
         nc.sync.dma_start(offsets[:], offs)
+
+        def listed(window, c0, c1):
+            return window.indirect(offsets[:, c0 // PER_COLUMN : c1 // PER_COLUMN])
+
         tab_sc = tile("tab_sc", [P, T // 4], I32)
         nc.gpsimd.memset(tab_sc[:], 0)
 
@@ -92,9 +95,9 @@ def tile_list_engram_dl_tier_addL_kernel(
         wv_raw.append(load_weight("wv", wv, 1))
         wkd_raw = [load_weight("wkd", wkd, a) for a in range(PASSES)]
 
-        nc.vector.tensor_copy(v_sc[0][:], tab_sc[:].bitcast(U8).indirect(offsets[:]))
+        nc.vector.tensor_copy(v_sc[0][:], listed(tab_sc[:].bitcast(U8), 0, J))
         nc.sync.dma_start(v_sc[1][0 : P - SHIFT, :].bitcast(I32), v_sc[0][SHIFT:P, :].bitcast(I32))
-        wk4_w = placed("wk4_w", [P, PASSES, 2 * N // 4], I32, 10240)
+        wk4_w = tile("wk4_w", [P, PASSES, 2 * N // 4], I32)
         nc.sync.dma_start(wk4_w[:], wk4_words.bitcast(I32).rearrange("a p c -> p a c"))
         for q in range(P // QUAD):
             nc.sync.dma_start(
@@ -102,64 +105,59 @@ def tile_list_engram_dl_tier_addL_kernel(
                 wk4_scales.bitcast(I32)[:, 4 * q : 4 * q + 4, :].rearrange("a r c -> r a c"),
             )
 
-        ke = [ps.tile([P, J], F32, name="ke%d" % h) for h in range(HALVES)]
-        ve = [ps.tile([P, J], F32, name="ve%d" % h) for h in range(HALVES)]
-        got_w = [tile("got_w%d" % u, [P, J // 2], I32) for u in range(2)]
-        for u in range(2):
-            nc.vector.tensor_copy(
-                got_w[u][:].bitcast(U32), tab_w[:].bitcast(U32).indirect(offsets[:, 16 * u : 16 * (u + 1)])
-            )
+        pieces = ((0, MID), (MID, J))
+        got_w = [tile("got_w%d" % u, [P, MID], I32) for u in range(len(pieces))]
+        for got, (c0, c1) in zip(got_w, pieces):
+            nc.vector.tensor_copy(got[:].bitcast(U32), listed(tab_w[:].bitcast(U32), c0, c1))
 
-        rec = [tile("rec%d" % h, [P, T], F32) for h in range(HALVES)]
         st_sb = [tile("st_sb%d" % h, [P, J], F32) for h in range(HALVES)]
-        nc.sync.dma_start(rec[0][:], rT[0:P, :])
+        rec = [tile("rec%d" % h, [P, T], F32) for h in range(HALVES)]
         for h in range(HALVES):
             nc.sync.dma_start(st_sb[h][:], st[h * P : (h + 1) * P, :])
-        nc.sync.dma_start(rec[1][:], rT[P : 2 * P, :])
+        for h in range(HALVES):
+            nc.sync.dma_start(rec[h][:], rT[h * P : (h + 1) * P, :])
 
         def interleaved(grouped):
-            return grouped.rearrange("p (c u i) -> p c i u", u=2, i=PACK)
+            return grouped.rearrange("p (c u i) -> p c i u", u=RUN, i=PACK)
 
         def rows_of(raw):
-            return raw.rearrange("p i (c u) -> p c i u", u=2)
+            return raw.rearrange("p i (c u) -> p c i u", u=RUN)
 
         def half(raw, h):
             return raw[:, :, h * P : (h + 1) * P]
 
-        def round_half(grouped, raw, h):
-            nc.scalar.copy(interleaved(grouped), rows_of(half(raw, h)))
+        def round_pass(grouped, raw):
+            for h in range(HALVES):
+                nc.scalar.copy(interleaved(grouped[h]), rows_of(half(raw, h)))
 
-        def table_pass(acc, words, scales, a, start, stop):
-            nc.tensor.matmul_mx(
-                acc[:], lhsT=words, lhsT_scale=scales,
-                rhs=v_w[:, a, :].bitcast(FP4X4), rhs_scale=v_sc[a][:],
-                start=start, stop=stop,
+        def operand(name, count_parts, words_tag="", scales_tag=""):
+            return (
+                tile(name + "_w", [P, count_parts * P], U32, words_tag),
+                tile(name + "_sc", [P, count_parts * P], U8, scales_tag),
             )
 
-        def operand(name):
-            return tile(name + "_w", [P, 4 * P], U32), tile(name + "_sc", [P, 4 * P], U8)
-
-        def blocks(w, first, count):
-            cols = slice(first * P, (first + count) * P)
+        def parts(w, first, count_parts=1):
+            cols = slice(first * P, (first + count_parts) * P)
             return w[0][:, cols].bitcast(FP8X4), w[1][:, cols]
 
-        def quantise(w, first, count, grouped):
-            nc.vector.quantize_mx(*blocks(w, first, count), grouped)
+        def rounded_tiles(name):
+            whole = tile(name + "0", [P, HALVES * K_PASS], BF16)
+            return whole, [tile("%s1%d" % (name, h), [P, K_PASS], BF16) for h in range(HALVES)]
+
+        def round_weight(whole, by_half, raw):
+            round_pass([whole[:, h * K_PASS : (h + 1) * K_PASS] for h in range(HALVES)], raw[0])
+            round_pass([t[:] for t in by_half], raw[1])
 
         warm = tile("warm", [P, 1], F32)
         nc.scalar.activation(warm[:], wv_raw[0][:, 0, 0:1], ACT.Sigmoid)
-        wv_bf0 = tile("wv_bf0", [P, HALVES, K_PASS], BF16)
-        wv_bf1 = [placed("wv_bf10", [P, K_PASS], BF16, 0), tile("wv_bf11", [P, K_PASS], BF16)]
-        for h in range(HALVES):
-            round_half(wv_bf0[:, h, :], wv_raw[0], h)
-        for h in range(HALVES):
-            round_half(wv_bf1[h][:], wv_raw[1], h)
+        wv_bf0, wv_bf1 = rounded_tiles("wv_bf")
+        round_weight(wv_bf0, wv_bf1, wv_raw)
 
-        wq, wd = operand("wq"), operand("wd")
+        wq, wd = operand("wq", PASSES * HALVES), operand("wd", PASSES * HALVES)
         back = {}
 
         def bring_back(a, h):
-            words, scales = blocks(wq, 2 * a + h, 1)
+            words, scales = parts(wq, 2 * a + h)
             bank = ps.tile([P, PACK, P], F32, name="back%d%d" % (a, h))
             for i in range(PACK):
                 sel = slice(i % 2 * P, (i % 2 + 1) * P)
@@ -169,93 +167,104 @@ def tile_list_engram_dl_tier_addL_kernel(
                 )
             back[a, h] = bank
 
-        quantise(wq, 0, 2, wv_bf0[:].rearrange("p h c -> p (h c)"))
+        nc.vector.quantize_mx(*parts(wq, 0, HALVES), wv_bf0[:])
         for h in range(HALVES):
             bring_back(0, h)
         v_w = tile("v_w", [P, PASSES, 2 * J], U8)
-        for u in range(2):
+        for got, (c0, c1) in zip(got_w, pieces):
             nc.vector.tensor_copy(
-                v_w[:].bitcast(U16)[:, :, u * J // 2 : (u + 1) * J // 2],
-                got_w[u][:].bitcast(U16).rearrange("p (j d) -> p d j", d=PASSES),
+                v_w[:].bitcast(U16)[:, :, c0:c1], got[:].bitcast(U16).rearrange("p (j d) -> p d j", d=PASSES)
             )
         for h in range(HALVES):
-            quantise(wq, 2 + h, 1, wv_bf1[h][:])
+            nc.vector.quantize_mx(*parts(wq, HALVES + h), wv_bf1[h][:])
             bring_back(1, h)
 
-        left = placed("left", [P, 3, K_PASS], BF16, 0)
-        wkd_bf0 = placed("wkd_bf0", [P, HALVES, K_PASS], BF16, 4096)
-        wkd_bf1 = [placed("wkd_bf10", [P, K_PASS], BF16, 6144), tile("wkd_bf11", [P, K_PASS], BF16)]
+        wkd_bf0, wkd_bf1 = rounded_tiles("wkd_bf")
+        round_weight(wkd_bf0, wkd_bf1, wkd_raw)
+        nc.vector.quantize_mx(*parts(wd, 0, HALVES), wkd_bf0[:])
         for h in range(HALVES):
-            round_half(wkd_bf0[:, h, :], wkd_raw[0], h)
-        for h in range(HALVES):
-            round_half(wkd_bf1[h][:], wkd_raw[1], h)
-        quantise(wd, 0, 2, wkd_bf0[:].rearrange("p a c -> p (a c)"))
-        for h in range(HALVES):
-            quantise(wd, 2 + h, 1, wkd_bf1[h][:])
-        for n, (a, h) in enumerate(((0, 0), (0, 1), (1, 0))):
+            nc.vector.quantize_mx(*parts(wd, HALVES + h), wkd_bf1[h][:])
+
+        on_vector = ((0, 0), (0, 1), (1, 0))
+        left = tile("left", [P, len(on_vector) * K_PASS], BF16, "wv_bf10")
+        for n, (a, h) in enumerate(on_vector):
             nc.vector.tensor_tensor(
-                interleaved(left[:, n, :]), rows_of(half(wv_raw[a], h)), rows_of(back[a, h][:]), ALU.subtract
+                interleaved(left[:, n * K_PASS : (n + 1) * K_PASS]),
+                rows_of(half(wv_raw[a], h)), rows_of(back[a, h][:]), ALU.subtract,
+            )
+
+        ke = [ps.tile([P, J], F32, name="ke%d" % h) for h in range(HALVES)]
+        ve = [ps.tile([P, J], F32, name="ve%d" % h) for h in range(HALVES)]
+
+        def table_pass(acc, words, scales, a, start=False, stop=False):
+            nc.tensor.matmul_mx(
+                acc[:], lhsT=words, lhsT_scale=scales,
+                rhs=v_w[:, a, :].bitcast(FP4X4), rhs_scale=v_sc[a][:], start=start, stop=stop,
             )
 
         for a in range(PASSES):
-            table_pass(ve[0], *blocks(wq, 2 * a, 1), a, a == 0, False)
+            table_pass(ve[0], *parts(wq, 2 * a), a, start=a == 0)
         for h in range(HALVES):
             for a in range(PASSES):
                 table_pass(
                     ke[h],
                     wk4_w[:, a, P // 2 * h : P // 2 * (h + 1)].bitcast(FP4X4),
                     wk4_sc[:, a, P // 4 * h : P // 4 * (h + 1)].bitcast(U8),
-                    a, a == 0, False,
+                    a, start=a == 0,
                 )
         for h in range(HALVES):
             for a in range(PASSES):
-                table_pass(ke[h], *blocks(wd, 2 * a + h, 1), a, False, a == PASSES - 1)
-        wr = tile("wr_w", [P, 3 * P], U32), placed("wr_sc", [P, 3 * P], U8, 10240)
-        quantise(wr, 0, 2, left[:, 0:2, :].rearrange("p a c -> p (a c)"))
-        quantise(wr, 2, 1, left[:, 2, :])
-        back_sb = placed("back_sb", [P, P, PACK], F32, 4096)
-        left_late = placed("left_late", [P, K_PASS], BF16, 0)
+                table_pass(ke[h], *parts(wd, 2 * a + h), a, stop=a == PASSES - 1)
+
+        wr = operand("wr", len(on_vector), scales_tag="wk4_w")
+        nc.vector.quantize_mx(*parts(wr, 0, HALVES), left[:, 0 : HALVES * K_PASS])
+        nc.vector.quantize_mx(*parts(wr, HALVES), left[:, HALVES * K_PASS : (HALVES + 1) * K_PASS])
+
+        back_sb = tile("back_sb", [P, P, PACK], F32, "wkd_bf0")
+        left_last = tile("left_last", [P, K_PASS], BF16, "wv_bf10")
         nc.scalar.copy(back_sb[:], back[1, 1][:].rearrange("p i c -> p c i"))
         nc.gpsimd.tensor_tensor(
-            left_late[:].rearrange("p (c i) -> p c i", i=PACK),
+            left_last[:].rearrange("p (c i) -> p c i", i=PACK),
             half(wv_raw[1], 1).rearrange("p i c -> p c i"), back_sb[:], ALU.subtract,
         )
         for a in range(PASSES):
-            table_pass(ve[0], *blocks(wr, 2 * a, 1), a, False, a == PASSES - 1)
+            table_pass(ve[0], *parts(wr, 2 * a), a, stop=a == PASSES - 1)
 
         pre = tile("pre", [P, HALVES, J], F32)
-        gate_first = placed("gate_first", [P, 256], F32, 8192)
-        gate = tile("gate", [P, HALVES, J], F32)
+        gate = {
+            (0, 0): tile("gate_first", [P, MID], F32)[:],
+            (0, MID): tile("gate_second", [P, MID], F32)[:],
+            (1, 0): tile("gate_third", [P, J], F32)[:],
+        }
         passed = tile("passed", [P, HALVES, J], F32)
         result = tile("result", [P, HALVES, J], F32)
-
-        def gate_of(h, c0, c1):
-            return gate_first[:] if (h, c0) == (0, 0) else gate[:, h, c0:c1]
-
-        for h, c0, c1 in ((0, 0, 256), (0, 256, J), (1, 0, J)):
+        for h, c0, c1 in ((0, 0, MID), (0, MID, J), (1, 0, J)):
             nc.vector.tensor_tensor(pre[:, h, c0:c1], ke[h][:, c0:c1], st_sb[h][:, c0:c1], ALU.add)
-            nc.scalar.activation(gate_of(h, c0, c1), pre[:, h, c0:c1], ACT.Sigmoid)
+            nc.scalar.activation(gate[h, c0], pre[:, h, c0:c1], ACT.Sigmoid)
 
-        def product(h, c0, c1):
-            nc.vector.tensor_tensor(passed[:, h, c0:c1], ve[h][:, c0:c1], gate_of(h, c0, c1), ALU.mult)
+        def product(h, c0, c1, gate_piece):
+            nc.vector.tensor_tensor(passed[:, h, c0:c1], ve[h][:, c0:c1], gate_piece, ALU.mult)
 
-        def finish(h, c0, c1):
-            nc.vector.tensor_tensor(
-                result[:, h, c0:c1], rec[h][:].indirect(offsets[:, c0 // 16 : c1 // 16]), passed[:, h, c0:c1], ALU.add
-            )
+        def add_record(h, c0, c1):
+            nc.vector.tensor_tensor(result[:, h, c0:c1], listed(rec[h][:], c0, c1), passed[:, h, c0:c1], ALU.add)
+
+        def store(h, c0, c1):
             nc.sync.dma_start(out[h * P : (h + 1) * P, c0:c1], result[:, h, c0:c1])
 
-        product(0, 0, 256)
-        product(0, 256, J)
-        late = placed("late_w", [P, P], U32, 8192), tile("late_sc", [P, P], U8)
-        quantise(late, 0, 1, left_late[:])
-        table_pass(ve[1], *blocks(wr, 1, 1), 0, True, False)
-        table_pass(ve[1], *blocks(wq, 1, 1), 0, False, False)
-        table_pass(ve[1], *blocks(wq, 3, 1), 1, False, False)
-        table_pass(ve[1], *blocks(late, 0, 1), 1, False, True)
-        finish(0, 0, 256)
-        finish(0, 256, J)
-        product(1, 0, 320)
-        product(1, 320, J)
-        finish(1, 0, 320)
-        finish(1, 320, J)
+        for c0, c1 in pieces:
+            product(0, c0, c1, gate[0, c0])
+        wr_last = operand("wr_last", 1, words_tag="gate_first")
+        nc.vector.quantize_mx(*parts(wr_last, 0), left_last[:])
+        table_pass(ve[1], *parts(wr, 1), 0, start=True)
+        for a in range(PASSES):
+            table_pass(ve[1], *parts(wq, 2 * a + 1), a)
+        table_pass(ve[1], *parts(wr_last, 0), 1, stop=True)
+        for c0, c1 in pieces:
+            add_record(0, c0, c1)
+        store(0, 0, J)
+        last_pieces = ((0, CUT), (CUT, J))
+        for c0, c1 in last_pieces:
+            product(1, c0, c1, gate[1, 0][:, c0:c1])
+        for c0, c1 in last_pieces:
+            add_record(1, c0, c1)
+            store(1, c0, c1)

@@ -93,17 +93,18 @@ def tile_list_engram_dl_tier_addL_kernel(
         tab_w = tile("tab_w", [P, T], I32)
         nc.sync.dma_start(tab_w[:], tab_words[0].rearrange("p t b -> p (t b)").bitcast(I32))
         wv_raw.append(load_weight("wv", wv, 1))
-        wkd_raw = [load_weight("wkd", wkd, a) for a in range(PASSES)]
-
-        nc.vector.tensor_copy(v_sc[0][:], listed(tab_sc[:].bitcast(U8), 0, J))
-        nc.sync.dma_start(v_sc[1][0 : P - SHIFT, :].bitcast(I32), v_sc[0][SHIFT:P, :].bitcast(I32))
-        wk4_w = tile("wk4_w", [P, PASSES, 2 * N // 4], I32)
-        nc.sync.dma_start(wk4_w[:], wk4_words.bitcast(I32).rearrange("a p c -> p a c"))
+        wkd_raw = [load_weight("wkd", wkd, 0)]
         for q in range(P // QUAD):
             nc.sync.dma_start(
                 wk4_sc[QUAD * q : QUAD * q + 4, :, :],
                 wk4_scales.bitcast(I32)[:, 4 * q : 4 * q + 4, :].rearrange("a r c -> r a c"),
             )
+        wkd_raw.append(load_weight("wkd", wkd, 1))
+
+        nc.vector.tensor_copy(v_sc[0][:], listed(tab_sc[:].bitcast(U8), 0, J))
+        nc.sync.dma_start(v_sc[1][0 : P - SHIFT, :].bitcast(I32), v_sc[0][SHIFT:P, :].bitcast(I32))
+        wk4_w = tile("wk4_w", [P, PASSES, 2 * N // 4], I32)
+        nc.sync.dma_start(wk4_w[:], wk4_words.bitcast(I32).rearrange("a p c -> p a c"))
 
         pieces = ((0, MID), (MID, J))
         got_w = [tile("got_w%d" % u, [P, MID], I32) for u in range(len(pieces))]
@@ -220,7 +221,7 @@ def tile_list_engram_dl_tier_addL_kernel(
         nc.vector.quantize_mx(*parts(wr, 0, HALVES), left[:, 0 : HALVES * K_PASS])
         nc.vector.quantize_mx(*parts(wr, HALVES), left[:, HALVES * K_PASS : (HALVES + 1) * K_PASS])
 
-        back_sb = tile("back_sb", [P, P, PACK], F32, "wkd_bf0")
+        back_sb = tile("back_sb", [P, P, PACK], F32, "wkd_bf10")
         left_last = tile("left_last", [P, K_PASS], BF16, "wv_bf10")
         nc.scalar.copy(back_sb[:], back[1, 1][:].rearrange("p i c -> p c i"))
         nc.gpsimd.tensor_tensor(

@@ -27,6 +27,7 @@ SHIFT = 16
 RUN = 2
 MID = J // 2
 CUT = 320
+SHARE = 112
 
 
 def tile_list_engram_dl_tier_addL_kernel(
@@ -48,6 +49,17 @@ def tile_list_engram_dl_tier_addL_kernel(
 
         tab_sc = tile("tab_sc", [P, T // 4], I32)
         nc.gpsimd.memset(tab_sc[:], 0)
+        wk4_sc = tile("wk4_sc", [P, PASSES, N // 4], I32)
+        nc.gpsimd.memset(wk4_sc[:], 0)
+
+        def load_wk4_scales(queue, q):
+            queue.dma_start(
+                wk4_sc[QUAD * q : QUAD * q + 4, :, :],
+                wk4_scales.bitcast(I32)[:, 4 * q : 4 * q + 4, :].rearrange("a r c -> r a c"),
+            )
+
+        for q in (0, 1):
+            load_wk4_scales(nc.gpsimd, q)
 
         ones = tile("ones", [P, QUAD], F32)
         nc.vector.memset(ones[:], 1.0)
@@ -55,9 +67,7 @@ def tile_list_engram_dl_tier_addL_kernel(
         nc.vector.memset(pick_in[:].bitcast(I32), 0)
         count = tile("count", [P, QUAD], F32)
         nc.vector.tensor_tensor_scan(count[:], ones[:], ones[:], 0.0, ALU.mult, ALU.add)
-        wk4_sc = tile("wk4_sc", [P, PASSES, N // 4], I32)
         v_sc = [tile("v_sc%d" % a, [P, J], U8) for a in range(PASSES)]
-        nc.vector.memset(wk4_sc[:], 0)
         own = tile("own", [P, QUAD], F32)
         nc.vector.transpose(own[:], count[:])
         nc.vector.memset(v_sc[1][:].bitcast(I32), 0)
@@ -94,29 +104,25 @@ def tile_list_engram_dl_tier_addL_kernel(
         nc.sync.dma_start(tab_w[:], tab_words[0].rearrange("p t b -> p (t b)").bitcast(I32))
         wv_raw.append(load_weight("wv", wv, 1))
         wkd_raw = [load_weight("wkd", wkd, 0)]
-        for q in range(P // QUAD):
-            nc.sync.dma_start(
-                wk4_sc[QUAD * q : QUAD * q + 4, :, :],
-                wk4_scales.bitcast(I32)[:, 4 * q : 4 * q + 4, :].rearrange("a r c -> r a c"),
-            )
         wkd_raw.append(load_weight("wkd", wkd, 1))
-
-        nc.vector.tensor_copy(v_sc[0][:], listed(tab_sc[:].bitcast(U8), 0, J))
-        nc.sync.dma_start(v_sc[1][0 : P - SHIFT, :].bitcast(I32), v_sc[0][SHIFT:P, :].bitcast(I32))
         wk4_w = tile("wk4_w", [P, PASSES, 2 * N // 4], I32)
         nc.sync.dma_start(wk4_w[:], wk4_words.bitcast(I32).rearrange("a p c -> p a c"))
+        for q in (2, 3):
+            load_wk4_scales(nc.sync, q)
+
+        nc.vector.tensor_copy(v_sc[0][:, 0:MID], listed(tab_sc[:].bitcast(U8), 0, MID))
 
         pieces = ((0, MID), (MID, J))
         got_w = [tile("got_w%d" % u, [P, MID], I32) for u in range(len(pieces))]
-        for got, (c0, c1) in zip(got_w, pieces):
-            nc.vector.tensor_copy(got[:].bitcast(U32), listed(tab_w[:].bitcast(U32), c0, c1))
 
         st_sb = [tile("st_sb%d" % h, [P, J], F32) for h in range(HALVES)]
         rec = [tile("rec%d" % h, [P, T], F32) for h in range(HALVES)]
-        for h in range(HALVES):
-            nc.sync.dma_start(st_sb[h][:], st[h * P : (h + 1) * P, :])
-        for h in range(HALVES):
-            nc.sync.dma_start(rec[h][:], rT[h * P : (h + 1) * P, :])
+
+        def load_late():
+            for h in range(HALVES):
+                nc.sync.dma_start(st_sb[h][:], st[h * P : (h + 1) * P, :])
+            for h in range(HALVES):
+                nc.sync.dma_start(rec[h][:], rT[h * P : (h + 1) * P, :])
 
         def interleaved(grouped):
             return grouped.rearrange("p (c u i) -> p c i u", u=RUN, i=PACK)
@@ -152,10 +158,25 @@ def tile_list_engram_dl_tier_addL_kernel(
         warm = tile("warm", [P, 1], F32)
         nc.scalar.activation(warm[:], wv_raw[0][:, 0, 0:1], ACT.Sigmoid)
         wv_bf0, wv_bf1 = rounded_tiles("wv_bf")
-        round_weight(wv_bf0, wv_bf1, wv_raw)
+        round_pass([wv_bf0[:, h * K_PASS : (h + 1) * K_PASS] for h in range(HALVES)], wv_raw[0])
 
-        wq, wd = operand("wq", PASSES * HALVES), operand("wd", PASSES * HALVES)
+        def by_column(raw):
+            return raw.rearrange("p i c -> p c i")
+
+        def columns(grouped):
+            return grouped.rearrange("p (c i) -> p c i", i=PACK)
+
+        nc.gpsimd.tensor_scalar(columns(wv_bf1[0][:]), by_column(half(wv_raw[1], 0)), 1.0, 0.0, ALU.mult, ALU.add)
+
+        wq = operand("wq", PASSES * HALVES)
         back = {}
+
+        spare = ps.tile([P, 2 * P], F32, name="spare", tag="ve1")
+        for u in range(3):
+            nc.tensor.matmul_mx(
+                spare[:], lhsT=pick_w[0][:, 0:P].bitcast(FP8X4), lhsT_scale=pick_sc[:, 0:P],
+                rhs=pick_w[0][:].bitcast(FP8X4), rhs_scale=tab_sc[:].bitcast(U8)[:, 0 : 2 * P], start=True, stop=True,
+            )
 
         def bring_back(a, h):
             words, scales = parts(wq, 2 * a + h)
@@ -168,9 +189,18 @@ def tile_list_engram_dl_tier_addL_kernel(
                 )
             back[a, h] = bank
 
-        nc.vector.quantize_mx(*parts(wq, 0, HALVES), wv_bf0[:])
         for h in range(HALVES):
+            nc.vector.quantize_mx(*parts(wq, h), wv_bf0[:, h * K_PASS : (h + 1) * K_PASS])
             bring_back(0, h)
+            if h == 0:
+                nc.vector.tensor_copy(v_sc[0][:, MID:J], listed(tab_sc[:].bitcast(U8), MID, J))
+                nc.sync.dma_start(v_sc[1][0 : P - SHIFT, :].bitcast(I32), v_sc[0][SHIFT:P, :].bitcast(I32))
+                load_late()
+        for got, (c0, c1) in zip(got_w, pieces):
+            nc.vector.tensor_copy(got[:].bitcast(U32), listed(tab_w[:].bitcast(U32), c0, c1))
+        back_first = tile("back_first", [P, SHARE, PACK], F32)
+        nc.scalar.copy(back_first[:], by_column(back[0, 0][:, :, 0:SHARE]))
+        nc.scalar.copy(interleaved(wv_bf1[1][:]), rows_of(half(wv_raw[1], 1)))
         v_w = tile("v_w", [P, PASSES, 2 * J], U8)
         for got, (c0, c1) in zip(got_w, pieces):
             nc.vector.tensor_copy(
@@ -180,22 +210,30 @@ def tile_list_engram_dl_tier_addL_kernel(
             nc.vector.quantize_mx(*parts(wq, HALVES + h), wv_bf1[h][:])
             bring_back(1, h)
 
+        wd = operand("wd", PASSES * HALVES)
         wkd_bf0, wkd_bf1 = rounded_tiles("wkd_bf")
         round_weight(wkd_bf0, wkd_bf1, wkd_raw)
         nc.vector.quantize_mx(*parts(wd, 0, HALVES), wkd_bf0[:])
         for h in range(HALVES):
             nc.vector.quantize_mx(*parts(wd, HALVES + h), wkd_bf1[h][:])
 
-        on_vector = ((0, 0), (0, 1), (1, 0))
-        left = tile("left", [P, len(on_vector) * K_PASS], BF16, "wv_bf10")
-        for n, (a, h) in enumerate(on_vector):
+        left0 = tile("left0", [P, HALVES * K_PASS], BF16, "wv_bf10")
+        left10 = tile("left10", [P, K_PASS], BF16)
+        nc.gpsimd.tensor_tensor(
+            columns(left0[:, 0 : SHARE * PACK]), by_column(wv_raw[0][:, :, 0:SHARE]), back_first[:], ALU.subtract
+        )
+
+        def subtract(left, a, h, c0=0):
             nc.vector.tensor_tensor(
-                interleaved(left[:, n * K_PASS : (n + 1) * K_PASS]),
-                rows_of(half(wv_raw[a], h)), rows_of(back[a, h][:]), ALU.subtract,
+                interleaved(left), rows_of(half(wv_raw[a], h)[:, :, c0:P]), rows_of(back[a, h][:, :, c0:P]), ALU.subtract
             )
 
+        subtract(left0[:, SHARE * PACK : K_PASS], 0, 0, SHARE)
+        subtract(left0[:, K_PASS : 2 * K_PASS], 0, 1)
+        subtract(left10[:], 1, 0)
+
         ke = [ps.tile([P, J], F32, name="ke%d" % h) for h in range(HALVES)]
-        ve = [ps.tile([P, J], F32, name="ve%d" % h) for h in range(HALVES)]
+        ve = [ps.tile([P, J], F32, name="ve%d" % h, tag="ve%d" % h) for h in range(HALVES)]
 
         def table_pass(acc, words, scales, a, start=False, stop=False):
             nc.tensor.matmul_mx(
@@ -203,10 +241,9 @@ def tile_list_engram_dl_tier_addL_kernel(
                 rhs=v_w[:, a, :].bitcast(FP4X4), rhs_scale=v_sc[a][:], start=start, stop=stop,
             )
 
+        table_pass(ve[0], *parts(wq, 0), 0, start=True)
         for a in range(PASSES):
-            table_pass(ve[0], *parts(wq, 2 * a), a, start=a == 0)
-        for h in range(HALVES):
-            for a in range(PASSES):
+            for h in range(HALVES):
                 table_pass(
                     ke[h],
                     wk4_w[:, a, P // 2 * h : P // 2 * (h + 1)].bitcast(FP4X4),
@@ -216,10 +253,11 @@ def tile_list_engram_dl_tier_addL_kernel(
         for h in range(HALVES):
             for a in range(PASSES):
                 table_pass(ke[h], *parts(wd, 2 * a + h), a, stop=a == PASSES - 1)
+        table_pass(ve[0], *parts(wq, 2), 1)
 
-        wr = operand("wr", len(on_vector), scales_tag="wk4_w")
-        nc.vector.quantize_mx(*parts(wr, 0, HALVES), left[:, 0 : HALVES * K_PASS])
-        nc.vector.quantize_mx(*parts(wr, HALVES), left[:, HALVES * K_PASS : (HALVES + 1) * K_PASS])
+        wr = operand("wr", HALVES + 1, scales_tag="wk4_w")
+        nc.vector.quantize_mx(*parts(wr, 0, HALVES), left0[:])
+        nc.vector.quantize_mx(*parts(wr, HALVES), left10[:])
 
         back_sb = tile("back_sb", [P, P, PACK], F32, "wkd_bf10")
         left_last = tile("left_last", [P, K_PASS], BF16, "wv_bf10")

@@ -49,17 +49,6 @@ def tile_list_engram_dl_tier_addL_kernel(
 
         tab_sc = tile("tab_sc", [P, T // 4], I32)
         nc.gpsimd.memset(tab_sc[:], 0)
-        wk4_sc = tile("wk4_sc", [P, PASSES, N // 4], I32)
-        nc.gpsimd.memset(wk4_sc[:], 0)
-
-        def load_wk4_scales(queue, q):
-            queue.dma_start(
-                wk4_sc[QUAD * q : QUAD * q + 4, :, :],
-                wk4_scales.bitcast(I32)[:, 4 * q : 4 * q + 4, :].rearrange("a r c -> r a c"),
-            )
-
-        for q in (0, 1):
-            load_wk4_scales(nc.gpsimd, q)
 
         ones = tile("ones", [P, QUAD], F32)
         nc.vector.memset(ones[:], 1.0)
@@ -67,7 +56,9 @@ def tile_list_engram_dl_tier_addL_kernel(
         nc.vector.memset(pick_in[:].bitcast(I32), 0)
         count = tile("count", [P, QUAD], F32)
         nc.vector.tensor_tensor_scan(count[:], ones[:], ones[:], 0.0, ALU.mult, ALU.add)
+        wk4_sc = tile("wk4_sc", [P, PASSES, N // 4], I32)
         v_sc = [tile("v_sc%d" % a, [P, J], U8) for a in range(PASSES)]
+        nc.vector.memset(wk4_sc[:], 0)
         own = tile("own", [P, QUAD], F32)
         nc.vector.transpose(own[:], count[:])
         nc.vector.memset(v_sc[1][:].bitcast(I32), 0)
@@ -104,11 +95,13 @@ def tile_list_engram_dl_tier_addL_kernel(
         nc.sync.dma_start(tab_w[:], tab_words[0].rearrange("p t b -> p (t b)").bitcast(I32))
         wv_raw.append(load_weight("wv", wv, 1))
         wkd_raw = [load_weight("wkd", wkd, 0)]
+        for q in range(P // QUAD):
+            nc.sync.dma_start(
+                wk4_sc[QUAD * q : QUAD * q + 4, :, :],
+                wk4_scales.bitcast(I32)[:, 4 * q : 4 * q + 4, :].rearrange("a r c -> r a c"),
+            )
         wkd_raw.append(load_weight("wkd", wkd, 1))
         wk4_w = tile("wk4_w", [P, PASSES, 2 * N // 4], I32)
-        nc.sync.dma_start(wk4_w[:], wk4_words.bitcast(I32).rearrange("a p c -> p a c"))
-        for q in (2, 3):
-            load_wk4_scales(nc.sync, q)
 
         nc.vector.tensor_copy(v_sc[0][:, 0:MID], listed(tab_sc[:].bitcast(U8), 0, MID))
 
@@ -119,6 +112,7 @@ def tile_list_engram_dl_tier_addL_kernel(
         rec = [tile("rec%d" % h, [P, T], F32) for h in range(HALVES)]
 
         def load_late():
+            nc.sync.dma_start(wk4_w[:], wk4_words.bitcast(I32).rearrange("a p c -> p a c"))
             for h in range(HALVES):
                 nc.sync.dma_start(st_sb[h][:], st[h * P : (h + 1) * P, :])
             for h in range(HALVES):
@@ -241,7 +235,8 @@ def tile_list_engram_dl_tier_addL_kernel(
                 rhs=v_w[:, a, :].bitcast(FP4X4), rhs_scale=v_sc[a][:], start=start, stop=stop,
             )
 
-        table_pass(ve[0], *parts(wq, 0), 0, start=True)
+        for a in range(PASSES):
+            table_pass(ve[0], *parts(wq, 2 * a), a, start=a == 0)
         for a in range(PASSES):
             for h in range(HALVES):
                 table_pass(
@@ -253,7 +248,6 @@ def tile_list_engram_dl_tier_addL_kernel(
         for h in range(HALVES):
             for a in range(PASSES):
                 table_pass(ke[h], *parts(wd, 2 * a + h), a, stop=a == PASSES - 1)
-        table_pass(ve[0], *parts(wq, 2), 1)
 
         wr = operand("wr", HALVES + 1, scales_tag="wk4_w")
         nc.vector.quantize_mx(*parts(wr, 0, HALVES), left0[:])

@@ -101,22 +101,13 @@ def tile_list_engram_dl_tier_addL_kernel(
                 wk4_scales.bitcast(I32)[:, 4 * q : 4 * q + 4, :].rearrange("a r c -> r a c"),
             )
         wkd_raw.append(load_weight("wkd", wkd, 1))
-        wk4_w = tile("wk4_w", [P, PASSES, 2 * N // 4], I32)
-
-        nc.vector.tensor_copy(v_sc[0][:, 0:MID], listed(tab_sc[:].bitcast(U8), 0, MID))
 
         pieces = ((0, MID), (MID, J))
-        got_w = [tile("got_w%d" % u, [P, MID], I32) for u in range(len(pieces))]
 
-        st_sb = [tile("st_sb%d" % h, [P, J], F32) for h in range(HALVES)]
-        rec = [tile("rec%d" % h, [P, T], F32) for h in range(HALVES)]
+        def gather_scales(c0, c1):
+            nc.vector.tensor_copy(v_sc[0][:, c0:c1], listed(tab_sc[:].bitcast(U8), c0, c1))
 
-        def load_late():
-            nc.sync.dma_start(wk4_w[:], wk4_words.bitcast(I32).rearrange("a p c -> p a c"))
-            for h in range(HALVES):
-                nc.sync.dma_start(st_sb[h][:], st[h * P : (h + 1) * P, :])
-            for h in range(HALVES):
-                nc.sync.dma_start(rec[h][:], rT[h * P : (h + 1) * P, :])
+        gather_scales(*pieces[0])
 
         def interleaved(grouped):
             return grouped.rearrange("p (c u i) -> p c i u", u=RUN, i=PACK)
@@ -126,6 +117,12 @@ def tile_list_engram_dl_tier_addL_kernel(
 
         def half(raw, h):
             return raw[:, :, h * P : (h + 1) * P]
+
+        def by_column(raw):
+            return raw.rearrange("p i c -> p c i")
+
+        def columns(grouped):
+            return grouped.rearrange("p (c i) -> p c i", i=PACK)
 
         def round_pass(grouped, raw):
             for h in range(HALVES):
@@ -145,32 +142,28 @@ def tile_list_engram_dl_tier_addL_kernel(
             whole = tile(name + "0", [P, HALVES * K_PASS], BF16)
             return whole, [tile("%s1%d" % (name, h), [P, K_PASS], BF16) for h in range(HALVES)]
 
-        def round_weight(whole, by_half, raw):
-            round_pass([whole[:, h * K_PASS : (h + 1) * K_PASS] for h in range(HALVES)], raw[0])
-            round_pass([t[:] for t in by_half], raw[1])
+        def halves_of(whole):
+            return [whole[:, h * K_PASS : (h + 1) * K_PASS] for h in range(HALVES)]
 
         warm = tile("warm", [P, 1], F32)
         nc.scalar.activation(warm[:], wv_raw[0][:, 0, 0:1], ACT.Sigmoid)
         wv_bf0, wv_bf1 = rounded_tiles("wv_bf")
-        round_pass([wv_bf0[:, h * K_PASS : (h + 1) * K_PASS] for h in range(HALVES)], wv_raw[0])
-
-        def by_column(raw):
-            return raw.rearrange("p i c -> p c i")
-
-        def columns(grouped):
-            return grouped.rearrange("p (c i) -> p c i", i=PACK)
-
+        round_pass(halves_of(wv_bf0), wv_raw[0])
         nc.gpsimd.tensor_scalar(columns(wv_bf1[0][:]), by_column(half(wv_raw[1], 0)), 1.0, 0.0, ALU.mult, ALU.add)
 
         wq = operand("wq", PASSES * HALVES)
         back = {}
 
-        spare = ps.tile([P, 2 * P], F32, name="spare", tag="ve1")
-        for u in range(3):
+        spare = ps.tile([P, J], F32, name="spare", tag="ve1")
+
+        def warm_up(count_columns, words, scales):
             nc.tensor.matmul_mx(
-                spare[:], lhsT=pick_w[0][:, 0:P].bitcast(FP8X4), lhsT_scale=pick_sc[:, 0:P],
-                rhs=pick_w[0][:].bitcast(FP8X4), rhs_scale=tab_sc[:].bitcast(U8)[:, 0 : 2 * P], start=True, stop=True,
+                spare[:, 0:count_columns], lhsT=pick_w[0][:, 0:P].bitcast(FP8X4), lhsT_scale=pick_sc[:, 0:P],
+                rhs=words, rhs_scale=scales, start=True, stop=True,
             )
+
+        for u in range(2):
+            warm_up(2 * P, pick_w[0][:].bitcast(FP8X4), tab_sc[:].bitcast(U8)[:, 0 : 2 * P])
 
         def bring_back(a, h):
             words, scales = parts(wq, 2 * a + h)
@@ -183,15 +176,25 @@ def tile_list_engram_dl_tier_addL_kernel(
                 )
             back[a, h] = bank
 
+        nc.vector.quantize_mx(*parts(wq, 0), halves_of(wv_bf0)[0])
+        bring_back(0, 0)
+        gather_scales(*pieces[1])
+        nc.sync.dma_start(v_sc[1][0 : P - SHIFT, :].bitcast(I32), v_sc[0][SHIFT:P, :].bitcast(I32))
+        wk4_w = tile("wk4_w", [P, PASSES, 2 * N // 4], I32)
+        nc.sync.dma_start(wk4_w[:], wk4_words.bitcast(I32).rearrange("a p c -> p a c"))
+        st_sb = [tile("st_sb%d" % h, [P, J], F32) for h in range(HALVES)]
+        rec = [tile("rec%d" % h, [P, T], F32) for h in range(HALVES)]
         for h in range(HALVES):
-            nc.vector.quantize_mx(*parts(wq, h), wv_bf0[:, h * K_PASS : (h + 1) * K_PASS])
-            bring_back(0, h)
-            if h == 0:
-                nc.vector.tensor_copy(v_sc[0][:, MID:J], listed(tab_sc[:].bitcast(U8), MID, J))
-                nc.sync.dma_start(v_sc[1][0 : P - SHIFT, :].bitcast(I32), v_sc[0][SHIFT:P, :].bitcast(I32))
-                load_late()
+            nc.sync.dma_start(st_sb[h][:], st[h * P : (h + 1) * P, :])
+        for h in range(HALVES):
+            nc.sync.dma_start(rec[h][:], rT[h * P : (h + 1) * P, :])
+        nc.vector.quantize_mx(*parts(wq, 1), halves_of(wv_bf0)[1])
+        bring_back(0, 1)
+
+        got_w = [tile("got_w%d" % u, [P, MID], I32) for u in range(len(pieces))]
         for got, (c0, c1) in zip(got_w, pieces):
             nc.vector.tensor_copy(got[:].bitcast(U32), listed(tab_w[:].bitcast(U32), c0, c1))
+        warm_up(J, got_w[0][:].bitcast(U8).bitcast(FP4X4), v_sc[0][:])
         back_first = tile("back_first", [P, SHARE, PACK], F32)
         nc.scalar.copy(back_first[:], by_column(back[0, 0][:, :, 0:SHARE]))
         nc.scalar.copy(interleaved(wv_bf1[1][:]), rows_of(half(wv_raw[1], 1)))
@@ -206,7 +209,8 @@ def tile_list_engram_dl_tier_addL_kernel(
 
         wd = operand("wd", PASSES * HALVES)
         wkd_bf0, wkd_bf1 = rounded_tiles("wkd_bf")
-        round_weight(wkd_bf0, wkd_bf1, wkd_raw)
+        round_pass(halves_of(wkd_bf0), wkd_raw[0])
+        round_pass([t[:] for t in wkd_bf1], wkd_raw[1])
         nc.vector.quantize_mx(*parts(wd, 0, HALVES), wkd_bf0[:])
         for h in range(HALVES):
             nc.vector.quantize_mx(*parts(wd, HALVES + h), wkd_bf1[h][:])
@@ -253,13 +257,10 @@ def tile_list_engram_dl_tier_addL_kernel(
         nc.vector.quantize_mx(*parts(wr, 0, HALVES), left0[:])
         nc.vector.quantize_mx(*parts(wr, HALVES), left10[:])
 
-        back_sb = tile("back_sb", [P, P, PACK], F32, "wkd_bf10")
+        back_last = tile("back_last", [P, P, PACK], F32, "wkd_bf10")
         left_last = tile("left_last", [P, K_PASS], BF16, "wv_bf10")
-        nc.scalar.copy(back_sb[:], back[1, 1][:].rearrange("p i c -> p c i"))
-        nc.gpsimd.tensor_tensor(
-            left_last[:].rearrange("p (c i) -> p c i", i=PACK),
-            half(wv_raw[1], 1).rearrange("p i c -> p c i"), back_sb[:], ALU.subtract,
-        )
+        nc.scalar.copy(back_last[:], by_column(back[1, 1][:]))
+        nc.gpsimd.tensor_tensor(columns(left_last[:]), by_column(half(wv_raw[1], 1)), back_last[:], ALU.subtract)
         for a in range(PASSES):
             table_pass(ve[0], *parts(wr, 2 * a), a, stop=a == PASSES - 1)
 

@@ -100,14 +100,14 @@ def tile_list_engram_dl_tier_addL_kernel(
                 wk4_sc[QUAD * q : QUAD * q + 4, :, :],
                 wk4_scales.bitcast(I32)[:, 4 * q : 4 * q + 4, :].rearrange("a r c -> r a c"),
             )
+        wk4_w = tile("wk4_w", [P, PASSES, 2 * N // 4], I32)
+        nc.sync.dma_start(wk4_w[:], wk4_words.bitcast(I32).rearrange("a p c -> p a c"))
         wkd_raw.append(load_weight("wkd", wkd, 1))
 
         pieces = ((0, MID), (MID, J))
 
         def gather_scales(c0, c1):
             nc.vector.tensor_copy(v_sc[0][:, c0:c1], listed(tab_sc[:].bitcast(U8), c0, c1))
-
-        gather_scales(*pieces[0])
 
         def interleaved(grouped):
             return grouped.rearrange("p (c u i) -> p c i u", u=RUN, i=PACK)
@@ -124,9 +124,8 @@ def tile_list_engram_dl_tier_addL_kernel(
         def columns(grouped):
             return grouped.rearrange("p (c i) -> p c i", i=PACK)
 
-        def round_pass(grouped, raw):
-            for h in range(HALVES):
-                nc.scalar.copy(interleaved(grouped[h]), rows_of(half(raw, h)))
+        def round_part(grouped, raw, h):
+            nc.scalar.copy(interleaved(grouped), rows_of(half(raw, h)))
 
         def operand(name, count_parts, words_tag="", scales_tag=""):
             return (
@@ -138,23 +137,18 @@ def tile_list_engram_dl_tier_addL_kernel(
             cols = slice(first * P, (first + count_parts) * P)
             return w[0][:, cols].bitcast(FP8X4), w[1][:, cols]
 
-        def rounded_tiles(name):
-            whole = tile(name + "0", [P, HALVES * K_PASS], BF16)
-            return whole, [tile("%s1%d" % (name, h), [P, K_PASS], BF16) for h in range(HALVES)]
-
-        def halves_of(whole):
-            return [whole[:, h * K_PASS : (h + 1) * K_PASS] for h in range(HALVES)]
+        gather_scales(*pieces[0])
 
         warm = tile("warm", [P, 1], F32)
         nc.scalar.activation(warm[:], wv_raw[0][:, 0, 0:1], ACT.Sigmoid)
-        wv_bf0, wv_bf1 = rounded_tiles("wv_bf")
-        round_pass(halves_of(wv_bf0), wv_raw[0])
-        nc.gpsimd.tensor_scalar(columns(wv_bf1[0][:]), by_column(half(wv_raw[1], 0)), 1.0, 0.0, ALU.mult, ALU.add)
+        wv_bf = {(a, h): tile("wv_bf%d%d" % (a, h), [P, K_PASS], BF16) for a in range(PASSES) for h in range(HALVES)}
+        round_part(wv_bf[0, 1][:], wv_raw[0], 1)
+        round_part(wv_bf[0, 0][:], wv_raw[0], 0)
+        nc.gpsimd.tensor_scalar(columns(wv_bf[1, 0][:]), by_column(half(wv_raw[1], 0)), 1.0, 0.0, ALU.mult, ALU.add)
 
         wq = operand("wq", PASSES * HALVES)
         back = {}
-
-        spare = ps.tile([P, J], F32, name="spare", tag="ve1")
+        spare = ps.tile([P, J], F32, name="spare")
 
         def warm_up(count_columns, words, scales):
             nc.tensor.matmul_mx(
@@ -165,8 +159,9 @@ def tile_list_engram_dl_tier_addL_kernel(
         for u in range(2):
             warm_up(2 * P, pick_w[0][:].bitcast(FP8X4), tab_sc[:].bitcast(U8)[:, 0 : 2 * P])
 
-        def bring_back(a, h):
+        def first_tier(a, h):
             words, scales = parts(wq, 2 * a + h)
+            nc.vector.quantize_mx(words, scales, wv_bf[a, h][:])
             bank = ps.tile([P, PACK, P], F32, name="back%d%d" % (a, h))
             for i in range(PACK):
                 sel = slice(i % 2 * P, (i % 2 + 1) * P)
@@ -176,93 +171,97 @@ def tile_list_engram_dl_tier_addL_kernel(
                 )
             back[a, h] = bank
 
-        nc.vector.quantize_mx(*parts(wq, 0), halves_of(wv_bf0)[0])
-        bring_back(0, 0)
+        first_tier(0, 1)
         gather_scales(*pieces[1])
         nc.sync.dma_start(v_sc[1][0 : P - SHIFT, :].bitcast(I32), v_sc[0][SHIFT:P, :].bitcast(I32))
-        wk4_w = tile("wk4_w", [P, PASSES, 2 * N // 4], I32)
-        nc.sync.dma_start(wk4_w[:], wk4_words.bitcast(I32).rearrange("a p c -> p a c"))
         st_sb = [tile("st_sb%d" % h, [P, J], F32) for h in range(HALVES)]
         rec = [tile("rec%d" % h, [P, T], F32) for h in range(HALVES)]
         for h in range(HALVES):
             nc.sync.dma_start(st_sb[h][:], st[h * P : (h + 1) * P, :])
         for h in range(HALVES):
             nc.sync.dma_start(rec[h][:], rT[h * P : (h + 1) * P, :])
-        nc.vector.quantize_mx(*parts(wq, 1), halves_of(wv_bf0)[1])
-        bring_back(0, 1)
+        first_tier(0, 0)
 
-        got_w = [tile("got_w%d" % u, [P, MID], I32) for u in range(len(pieces))]
-        for got, (c0, c1) in zip(got_w, pieces):
-            nc.vector.tensor_copy(got[:].bitcast(U32), listed(tab_w[:].bitcast(U32), c0, c1))
-        warm_up(J, got_w[0][:].bitcast(U8).bitcast(FP4X4), v_sc[0][:])
+        got_w = tile("got_w", [P, J], U32)
+        for c0, c1 in pieces:
+            nc.vector.tensor_copy(got_w[:, c0:c1], listed(tab_w[:].bitcast(U32), c0, c1))
+        warm_up(J, got_w[:, 0:MID].bitcast(U8).bitcast(FP4X4), v_sc[0][:])
+
+        def pass_words(a):
+            return got_w[:].bitcast(U16).rearrange("p (j d) -> p d j", d=PASSES)[:, a, :]
+
         back_first = tile("back_first", [P, SHARE, PACK], F32)
-        nc.scalar.copy(back_first[:], by_column(back[0, 0][:, :, 0:SHARE]))
-        nc.scalar.copy(interleaved(wv_bf1[1][:]), rows_of(half(wv_raw[1], 1)))
-        v_w = tile("v_w", [P, PASSES, 2 * J], U8)
-        for got, (c0, c1) in zip(got_w, pieces):
-            nc.vector.tensor_copy(
-                v_w[:].bitcast(U16)[:, :, c0:c1], got[:].bitcast(U16).rearrange("p (j d) -> p d j", d=PASSES)
-            )
-        for h in range(HALVES):
-            nc.vector.quantize_mx(*parts(wq, HALVES + h), wv_bf1[h][:])
-            bring_back(1, h)
+        nc.scalar.copy(back_first[:], by_column(back[0, 1][:, :, 0:SHARE]))
+        round_part(wv_bf[1, 1][:], wv_raw[1], 1)
+        v_w = [tile("v_w0", [P, 2 * J], U8)]
+        for c0, c1 in pieces:
+            nc.vector.tensor_copy(v_w[0][:].bitcast(U16)[:, c0:c1], pass_words(0)[:, c0:c1])
 
-        wd = operand("wd", PASSES * HALVES)
-        wkd_bf0, wkd_bf1 = rounded_tiles("wkd_bf")
-        round_pass(halves_of(wkd_bf0), wkd_raw[0])
-        round_pass([t[:] for t in wkd_bf1], wkd_raw[1])
-        nc.vector.quantize_mx(*parts(wd, 0, HALVES), wkd_bf0[:])
-        for h in range(HALVES):
-            nc.vector.quantize_mx(*parts(wd, HALVES + h), wkd_bf1[h][:])
-
-        left0 = tile("left0", [P, HALVES * K_PASS], BF16, "wv_bf10")
-        left10 = tile("left10", [P, K_PASS], BF16)
-        nc.gpsimd.tensor_tensor(
-            columns(left0[:, 0 : SHARE * PACK]), by_column(wv_raw[0][:, :, 0:SHARE]), back_first[:], ALU.subtract
-        )
-
-        def subtract(left, a, h, c0=0):
-            nc.vector.tensor_tensor(
-                interleaved(left), rows_of(half(wv_raw[a], h)[:, :, c0:P]), rows_of(back[a, h][:, :, c0:P]), ALU.subtract
-            )
-
-        subtract(left0[:, SHARE * PACK : K_PASS], 0, 0, SHARE)
-        subtract(left0[:, K_PASS : 2 * K_PASS], 0, 1)
-        subtract(left10[:], 1, 0)
-
-        ke = [ps.tile([P, J], F32, name="ke%d" % h) for h in range(HALVES)]
-        ve = [ps.tile([P, J], F32, name="ve%d" % h, tag="ve%d" % h) for h in range(HALVES)]
+        ke = [ps.tile([P, J], F32, name="ke%d" % h, tag="ke%d" % h) for h in range(HALVES)]
+        ve0 = ps.tile([P, J], F32, name="ve0")
 
         def table_pass(acc, words, scales, a, start=False, stop=False):
             nc.tensor.matmul_mx(
                 acc[:], lhsT=words, lhsT_scale=scales,
-                rhs=v_w[:, a, :].bitcast(FP4X4), rhs_scale=v_sc[a][:], start=start, stop=stop,
+                rhs=v_w[a][:].bitcast(FP4X4), rhs_scale=v_sc[a][:], start=start, stop=stop,
             )
 
-        for a in range(PASSES):
-            table_pass(ve[0], *parts(wq, 2 * a), a, start=a == 0)
+        def base_pass(a, h):
+            table_pass(
+                ke[h],
+                wk4_w[:, a, P // 2 * h : P // 2 * (h + 1)].bitcast(FP4X4),
+                wk4_sc[:, a, P // 4 * h : P // 4 * (h + 1)].bitcast(U8),
+                a, start=a == 0,
+            )
+
+        table_pass(ve0, *parts(wq, 0), 0, start=True)
+        for h in range(HALVES):
+            first_tier(1, h)
+        v_w.append(tile("v_w1", [P, 2 * J], U8, "wv_bf10"))
+        nc.vector.tensor_copy(v_w[1][:].bitcast(U16), pass_words(1))
+
+        left = tile("left", [P, 3, K_PASS], BF16, "wv_bf11")
+        nc.gpsimd.tensor_tensor(
+            columns(left[:, 2, 0 : SHARE * PACK]), by_column(half(wv_raw[0], 1)[:, :, 0:SHARE]), back_first[:], ALU.subtract
+        )
+
+        def subtract(dst, a, h, c0=0):
+            nc.vector.tensor_tensor(
+                interleaved(dst), rows_of(half(wv_raw[a], h)[:, :, c0:P]), rows_of(back[a, h][:, :, c0:P]), ALU.subtract
+            )
+
+        subtract(left[:, 0, :], 0, 0)
+        subtract(left[:, 1, :], 1, 0)
+        subtract(left[:, 2, SHARE * PACK : K_PASS], 0, 1, SHARE)
+
+        wd = operand("wd", PASSES * HALVES)
+        wkd_bf0 = tile("wkd_bf0", [P, HALVES, K_PASS], BF16)
+        wkd_bf1 = [tile("wkd_bf1%d" % h, [P, K_PASS], BF16) for h in range(HALVES)]
+        for h in range(HALVES):
+            round_part(wkd_bf0[:, h, :], wkd_raw[0], h)
+        for h in range(HALVES):
+            round_part(wkd_bf1[h][:], wkd_raw[1], h)
+        nc.vector.quantize_mx(*parts(wd, 0, HALVES), wkd_bf0[:].rearrange("p h f -> p (h f)"))
+        nc.vector.quantize_mx(*parts(wd, HALVES), wkd_bf1[0][:])
+
         for a in range(PASSES):
             for h in range(HALVES):
-                table_pass(
-                    ke[h],
-                    wk4_w[:, a, P // 2 * h : P // 2 * (h + 1)].bitcast(FP4X4),
-                    wk4_sc[:, a, P // 4 * h : P // 4 * (h + 1)].bitcast(U8),
-                    a, start=a == 0,
-                )
+                base_pass(a, h)
+        table_pass(ve0, *parts(wq, 2), 1)
+        wr = operand("wr", 3, scales_tag="wk4_w")
+        nc.vector.quantize_mx(*parts(wr, 0, 2), left[:, 0:2, :].rearrange("p h f -> p (h f)"))
+        nc.vector.quantize_mx(*parts(wd, HALVES + 1), wkd_bf1[1][:])
+        nc.vector.quantize_mx(*parts(wr, 2), left[:, 2, :])
         for h in range(HALVES):
             for a in range(PASSES):
                 table_pass(ke[h], *parts(wd, 2 * a + h), a, stop=a == PASSES - 1)
-
-        wr = operand("wr", HALVES + 1, scales_tag="wk4_w")
-        nc.vector.quantize_mx(*parts(wr, 0, HALVES), left0[:])
-        nc.vector.quantize_mx(*parts(wr, HALVES), left10[:])
+        for a in range(PASSES):
+            table_pass(ve0, *parts(wr, a), a, stop=a == PASSES - 1)
 
         back_last = tile("back_last", [P, P, PACK], F32, "wkd_bf10")
-        left_last = tile("left_last", [P, K_PASS], BF16, "wv_bf10")
+        left_last = tile("left_last", [P, K_PASS], BF16, "wv_bf11")
         nc.scalar.copy(back_last[:], by_column(back[1, 1][:]))
         nc.gpsimd.tensor_tensor(columns(left_last[:]), by_column(half(wv_raw[1], 1)), back_last[:], ALU.subtract)
-        for a in range(PASSES):
-            table_pass(ve[0], *parts(wr, 2 * a), a, stop=a == PASSES - 1)
 
         pre = tile("pre", [P, HALVES, J], F32)
         gate = {
@@ -276,6 +275,8 @@ def tile_list_engram_dl_tier_addL_kernel(
             nc.vector.tensor_tensor(pre[:, h, c0:c1], ke[h][:, c0:c1], st_sb[h][:, c0:c1], ALU.add)
             nc.scalar.activation(gate[h, c0], pre[:, h, c0:c1], ACT.Sigmoid)
 
+        ve = [ve0, ps.tile([P, J], F32, name="ve1", tag="ke0")]
+
         def product(h, c0, c1, gate_piece):
             nc.vector.tensor_tensor(passed[:, h, c0:c1], ve[h][:, c0:c1], gate_piece, ALU.mult)
 
@@ -285,13 +286,13 @@ def tile_list_engram_dl_tier_addL_kernel(
         def store(h, c0, c1):
             nc.sync.dma_start(out[h * P : (h + 1) * P, c0:c1], result[:, h, c0:c1])
 
+        for a in range(PASSES):
+            table_pass(ve[1], *parts(wq, 2 * a + 1), a, start=a == 0)
+        table_pass(ve[1], *parts(wr, 2), 0)
         for c0, c1 in pieces:
             product(0, c0, c1, gate[0, c0])
         wr_last = operand("wr_last", 1, words_tag="gate_first")
         nc.vector.quantize_mx(*parts(wr_last, 0), left_last[:])
-        table_pass(ve[1], *parts(wr, 1), 0, start=True)
-        for a in range(PASSES):
-            table_pass(ve[1], *parts(wq, 2 * a + 1), a)
         table_pass(ve[1], *parts(wr_last, 0), 1, stop=True)
         for c0, c1 in pieces:
             add_record(0, c0, c1)

@@ -148,16 +148,6 @@ def tile_list_engram_dl_tier_addL_kernel(
 
         wq = operand("wq", PASSES * HALVES)
         back = {}
-        spare = ps.tile([P, J], F32, name="spare")
-
-        def warm_up(count_columns, words, scales):
-            nc.tensor.matmul_mx(
-                spare[:, 0:count_columns], lhsT=pick_w[0][:, 0:P].bitcast(FP8X4), lhsT_scale=pick_sc[:, 0:P],
-                rhs=words, rhs_scale=scales, start=True, stop=True,
-            )
-
-        for u in range(2):
-            warm_up(2 * P, pick_w[0][:].bitcast(FP8X4), tab_sc[:].bitcast(U8)[:, 0 : 2 * P])
 
         def first_tier(a, h):
             words, scales = parts(wq, 2 * a + h)
@@ -185,7 +175,6 @@ def tile_list_engram_dl_tier_addL_kernel(
         got_w = tile("got_w", [P, J], U32)
         for c0, c1 in pieces:
             nc.vector.tensor_copy(got_w[:, c0:c1], listed(tab_w[:].bitcast(U32), c0, c1))
-        warm_up(J, got_w[:, 0:MID].bitcast(U8).bitcast(FP4X4), v_sc[0][:])
 
         def pass_words(a):
             return got_w[:].bitcast(U16).rearrange("p (j d) -> p d j", d=PASSES)[:, a, :]

from contextlib import ExitStack

import concourse.mybir as mybir

K, N, T, J = 1024, 256, 1024, 512
FLOPS = 1342177280

F32 = mybir.dt.float32
BF16 = mybir.dt.bfloat16
I32 = mybir.dt.int32
U32 = mybir.dt.uint32
U16 = mybir.dt.uint16
U8 = mybir.dt.uint8
FP8X4 = mybir.dt.float8_e4m3fn_x4
FP4X4 = mybir.dt.float4_e2m1fn_x4
ALU = mybir.AluOpType
ACT = mybir.ActivationFunctionType

P = 128
QUAD = 32
PACK = 4
K_PASS = P * PACK
PASSES = K // K_PASS
HALVES = N // P
PER_COLUMN = 16
SHIFT = 16
RUN = 2
MID = J // 2
CUT = 320
SHARE = 112


def tile_list_engram_dl_tier_addL_kernel(
    tc, tab_words, tab_scales, wk4_words, wk4_scales, wkd, wv, st, rT, offs, out
):
    nc = tc.nc
    with ExitStack() as ctx:
        sb = ctx.enter_context(tc.tile_pool(name="sb", bufs=1))
        ps = ctx.enter_context(tc.psum_pool(name="ps", bufs=1))

        def tile(name, shape, dtype, tag=""):
            return sb.tile(shape, dtype, name=name, tag=tag or name, align_bytes=64)

        offsets = sb.tile([P, J // PER_COLUMN], U16, name="offsets")
        nc.sync.dma_start(offsets[:], offs)

        def listed(window, c0, c1):
            return window.indirect(offsets[:, c0 // PER_COLUMN : c1 // PER_COLUMN])

        tab_sc = tile("tab_sc", [P, T // 4], I32)
        nc.gpsimd.memset(tab_sc[:], 0)

        ones = tile("ones", [P, QUAD], F32)
        nc.vector.memset(ones[:], 1.0)
        pick_in = tile("pick_in", [P, 2 * (K_PASS + 1)], BF16)
        nc.vector.memset(pick_in[:].bitcast(I32), 0)
        count = tile("count", [P, QUAD], F32)
        nc.vector.tensor_tensor_scan(count[:], ones[:], ones[:], 0.0, ALU.mult, ALU.add)
        wk4_sc = tile("wk4_sc", [P, PASSES, N // 4], I32)
        v_sc = [tile("v_sc%d" % a, [P, J], U8) for a in range(PASSES)]
        nc.vector.memset(wk4_sc[:], 0)
        own = tile("own", [P, QUAD], F32)
        nc.vector.transpose(own[:], count[:])
        nc.vector.memset(v_sc[1][:].bitcast(I32), 0)

        diagonals = pick_in[:].rearrange("p (i r) -> p i r", i=2)
        for b in range(P // QUAD):
            rows = slice(QUAD * b, QUAD * (b + 1))
            nc.vector.tensor_scalar(
                diagonals[rows, :, P * b : P * (b + 1) : PACK],
                count[rows, :].unsqueeze(1).to_broadcast([QUAD, 2, QUAD]),
                own[rows, 0:1], None, ALU.is_equal,
            )
        pick_w = [tile("pick_w%d" % u, [P, 2 * P], U32) for u in range(2)]
        pick_sc = tile("pick_sc", [P, 2 * P], U8)
        nc.vector.quantize_mx(pick_w[0][:].bitcast(FP8X4), pick_sc[:], pick_in[:, 0 : 2 * K_PASS])
        nc.vector.tensor_copy(
            pick_w[1][:].bitcast(U16).rearrange("p (w x) -> p w x", x=2),
            pick_w[0][:].bitcast(U16).rearrange("p (w x) -> p w x", x=2)[:, :, ::-1],
        )

        def load_weight(name, w, a):
            raw = tile("%s_raw%d" % (name, a), [P, PACK, N], F32)
            nc.sync.dma_start(
                raw[:], w[a * K_PASS : (a + 1) * K_PASS, :].rearrange("(p i) n -> p i n", i=PACK)
            )
            return raw

        wv_raw = [load_weight("wv", wv, 0)]
        for r in range(4):
            nc.sync.dma_start(
                tab_sc[r:P:SHIFT, :], tab_scales.bitcast(I32)[:, r:16:4, :].rearrange("a q c -> q a c")
            )
        tab_w = tile("tab_w", [P, T], I32)
        nc.sync.dma_start(tab_w[:], tab_words[0].rearrange("p t b -> p (t b)").bitcast(I32))
        wv_raw.append(load_weight("wv", wv, 1))
        wkd_raw = [load_weight("wkd", wkd, 0)]
        for q in range(P // QUAD):
            nc.sync.dma_start(
                wk4_sc[QUAD * q : QUAD * q + 4, :, :],
                wk4_scales.bitcast(I32)[:, 4 * q : 4 * q + 4, :].rearrange("a r c -> r a c"),
            )
        wk4_w = tile("wk4_w", [P, PASSES, 2 * N // 4], I32)
        nc.sync.dma_start(wk4_w[:], wk4_words.bitcast(I32).rearrange("a p c -> p a c"))
        wkd_raw.append(load_weight("wkd", wkd, 1))

        pieces = ((0, MID), (MID, J))

        def gather_scales(c0, c1):
            nc.vector.tensor_copy(v_sc[0][:, c0:c1], listed(tab_sc[:].bitcast(U8), c0, c1))

        def interleaved(grouped):
            return grouped.rearrange("p (c u i) -> p c i u", u=RUN, i=PACK)

        def rows_of(raw):
            return raw.rearrange("p i (c u) -> p c i u", u=RUN)

        def half(raw, h):
            return raw[:, :, h * P : (h + 1) * P]

        def by_column(raw):
            return raw.rearrange("p i c -> p c i")

        def columns(grouped):
            return grouped.rearrange("p (c i) -> p c i", i=PACK)

        def round_part(grouped, raw, h):
            nc.scalar.copy(interleaved(grouped), rows_of(half(raw, h)))

        def operand(name, count_parts, words_tag="", scales_tag=""):
            return (
                tile(name + "_w", [P, count_parts * P], U32, words_tag),
                tile(name + "_sc", [P, count_parts * P], U8, scales_tag),
            )

        def parts(w, first, count_parts=1):
            cols = slice(first * P, (first + count_parts) * P)
            return w[0][:, cols].bitcast(FP8X4), w[1][:, cols]

        gather_scales(*pieces[0])

        warm = tile("warm", [P, 1], F32)
        nc.scalar.activation(warm[:], wv_raw[0][:, 0, 0:1], ACT.Sigmoid)
        wv_bf = {(a, h): tile("wv_bf%d%d" % (a, h), [P, K_PASS], BF16) for a in range(PASSES) for h in range(HALVES)}
        round_part(wv_bf[0, 1][:], wv_raw[0], 1)
        round_part(wv_bf[0, 0][:], wv_raw[0], 0)
        nc.gpsimd.tensor_scalar(columns(wv_bf[1, 0][:]), by_column(half(wv_raw[1], 0)), 1.0, 0.0, ALU.mult, ALU.add)

        wq = operand("wq", PASSES * HALVES)
        back = {}

        def first_tier(a, h):
            words, scales = parts(wq, 2 * a + h)
            nc.vector.quantize_mx(words, scales, wv_bf[a, h][:])
            bank = ps.tile([P, PACK, P], F32, name="back%d%d" % (a, h))
            for i in range(PACK):
                sel = slice(i % 2 * P, (i % 2 + 1) * P)
                nc.tensor.matmul_mx(
                    bank[:, i, :], lhsT=pick_w[i // 2][:, sel].bitcast(FP8X4), lhsT_scale=pick_sc[:, sel],
                    rhs=words, rhs_scale=scales, start=True, stop=True,
                )
            back[a, h] = bank

        first_tier(0, 1)
        gather_scales(*pieces[1])
        nc.sync.dma_start(v_sc[1][0 : P - SHIFT, :].bitcast(I32), v_sc[0][SHIFT:P, :].bitcast(I32))
        st_sb = [tile("st_sb%d" % h, [P, J], F32) for h in range(HALVES)]
        rec = [tile("rec%d" % h, [P, T], F32) for h in range(HALVES)]
        for h in range(HALVES):
            nc.sync.dma_start(st_sb[h][:], st[h * P : (h + 1) * P, :])
        for h in range(HALVES):
            nc.sync.dma_start(rec[h][:], rT[h * P : (h + 1) * P, :])
        first_tier(0, 0)

        got_w = tile("got_w", [P, J], U32)
        for c0, c1 in pieces:
            nc.vector.tensor_copy(got_w[:, c0:c1], listed(tab_w[:].bitcast(U32), c0, c1))

        def pass_words(a):
            return got_w[:].bitcast(U16).rearrange("p (j d) -> p d j", d=PASSES)[:, a, :]

        back_first = tile("back_first", [P, SHARE, PACK], F32)
        nc.scalar.copy(back_first[:], by_column(back[0, 1][:, :, 0:SHARE]))
        round_part(wv_bf[1, 1][:], wv_raw[1], 1)
        v_w = [tile("v_w0", [P, 2 * J], U8)]
        for c0, c1 in pieces:
            nc.vector.tensor_copy(v_w[0][:].bitcast(U16)[:, c0:c1], pass_words(0)[:, c0:c1])

        ke = [ps.tile([P, J], F32, name="ke%d" % h, tag="ke%d" % h) for h in range(HALVES)]
        ve0 = ps.tile([P, J], F32, name="ve0")

        def table_pass(acc, words, scales, a, start=False, stop=False):
            nc.tensor.matmul_mx(
                acc[:], lhsT=words, lhsT_scale=scales,
                rhs=v_w[a][:].bitcast(FP4X4), rhs_scale=v_sc[a][:], start=start, stop=stop,
            )

        def base_pass(a, h):
            table_pass(
                ke[h],
                wk4_w[:, a, P // 2 * h : P // 2 * (h + 1)].bitcast(FP4X4),
                wk4_sc[:, a, P // 4 * h : P // 4 * (h + 1)].bitcast(U8),
                a, start=a == 0,
            )

        table_pass(ve0, *parts(wq, 0), 0, start=True)
        for h in range(HALVES):
            first_tier(1, h)
        v_w.append(tile("v_w1", [P, 2 * J], U8, "wv_bf10"))
        nc.vector.tensor_copy(v_w[1][:].bitcast(U16), pass_words(1))

        left = tile("left", [P, 3, K_PASS], BF16, "wv_bf11")
        nc.gpsimd.tensor_tensor(
            columns(left[:, 2, 0 : SHARE * PACK]), by_column(half(wv_raw[0], 1)[:, :, 0:SHARE]), back_first[:], ALU.subtract
        )

        def subtract(dst, a, h, c0=0):
            nc.vector.tensor_tensor(
                interleaved(dst), rows_of(half(wv_raw[a], h)[:, :, c0:P]), rows_of(back[a, h][:, :, c0:P]), ALU.subtract
            )

        subtract(left[:, 0, :], 0, 0)
        subtract(left[:, 1, :], 1, 0)
        subtract(left[:, 2, SHARE * PACK : K_PASS], 0, 1, SHARE)

        wd = operand("wd", PASSES * HALVES)
        wkd_bf0 = tile("wkd_bf0", [P, HALVES, K_PASS], BF16)
        wkd_bf1 = [tile("wkd_bf1%d" % h, [P, K_PASS], BF16) for h in range(HALVES)]
        for h in range(HALVES):
            round_part(wkd_bf0[:, h, :], wkd_raw[0], h)
        for h in range(HALVES):
            round_part(wkd_bf1[h][:], wkd_raw[1], h)
        nc.vector.quantize_mx(*parts(wd, 0, HALVES), wkd_bf0[:].rearrange("p h f -> p (h f)"))
        nc.vector.quantize_mx(*parts(wd, HALVES), wkd_bf1[0][:])

        for a in range(PASSES):
            for h in range(HALVES):
                base_pass(a, h)
        table_pass(ve0, *parts(wq, 2), 1)
        wr = operand("wr", 3, scales_tag="wk4_w")
        nc.vector.quantize_mx(*parts(wr, 0, 2), left[:, 0:2, :].rearrange("p h f -> p (h f)"))
        nc.vector.quantize_mx(*parts(wd, HALVES + 1), wkd_bf1[1][:])
        nc.vector.quantize_mx(*parts(wr, 2), left[:, 2, :])
        for h in range(HALVES):
            for a in range(PASSES):
                table_pass(ke[h], *parts(wd, 2 * a + h), a, stop=a == PASSES - 1)
        for a in range(PASSES):
            table_pass(ve0, *parts(wr, a), a, stop=a == PASSES - 1)

        back_last = tile("back_last", [P, P, PACK], F32, "wkd_bf10")
        left_last = tile("left_last", [P, K_PASS], BF16, "wv_bf11")
        nc.scalar.copy(back_last[:], by_column(back[1, 1][:]))
        nc.gpsimd.tensor_tensor(columns(left_last[:]), by_column(half(wv_raw[1], 1)), back_last[:], ALU.subtract)

        pre = tile("pre", [P, HALVES, J], F32)
        gate = {
            (0, 0): tile("gate_first", [P, MID], F32)[:],
            (0, MID): tile("gate_second", [P, MID], F32)[:],
            (1, 0): tile("gate_third", [P, J], F32)[:],
        }
        passed = tile("passed", [P, HALVES, J], F32)
        result = tile("result", [P, HALVES, J], F32)
        for h, c0, c1 in ((0, 0, MID), (0, MID, J), (1, 0, J)):
            nc.vector.tensor_tensor(pre[:, h, c0:c1], ke[h][:, c0:c1], st_sb[h][:, c0:c1], ALU.add)
            nc.scalar.activation(gate[h, c0], pre[:, h, c0:c1], ACT.Sigmoid)

        ve = [ve0, ps.tile([P, J], F32, name="ve1", tag="ke0")]

        def product(h, c0, c1, gate_piece):
            nc.vector.tensor_tensor(passed[:, h, c0:c1], ve[h][:, c0:c1], gate_piece, ALU.mult)

        def add_record(h, c0, c1):
            nc.vector.tensor_tensor(result[:, h, c0:c1], listed(rec[h][:], c0, c1), passed[:, h, c0:c1], ALU.add)

        def store(h, c0, c1):
            nc.sync.dma_start(out[h * P : (h + 1) * P, c0:c1], result[:, h, c0:c1])

        for a in range(PASSES):
            table_pass(ve[1], *parts(wq, 2 * a + 1), a, start=a == 0)
        table_pass(ve[1], *parts(wr, 2), 0)
        for c0, c1 in pieces:
            product(0, c0, c1, gate[0, c0])
        wr_last = operand("wr_last", 1, words_tag="gate_first")
        nc.vector.quantize_mx(*parts(wr_last, 0), left_last[:])
        table_pass(ve[1], *parts(wr_last, 0), 1, stop=True)
        for c0, c1 in pieces:
            add_record(0, c0, c1)
        store(0, 0, J)
        last_pieces = ((0, CUT), (CUT, J))
        for c0, c1 in last_pieces:
            product(1, c0, c1, gate[1, 0][:, c0:c1])
        for c0, c1 in last_pieces:
            add_record(1, c0, c1)
            store(1, c0, c1)
